import numpy as np
import ml_dtypes


def mxq(x, axis, fmt="e4m3"):
    dtype, down = {"e4m3": (ml_dtypes.float8_e4m3fn, 7), "e5m2": (ml_dtypes.float8_e5m2, 14)}[fmt]
    v = np.moveaxis(np.asarray(x, np.float32).astype(ml_dtypes.bfloat16).astype(np.float64), axis, -1)
    blocks = v.reshape(v.shape[:-1] + (-1, 32))
    amax = np.abs(blocks).max(-1, keepdims=True)
    byte = np.maximum(np.where(amax > 0, np.frexp(amax)[1] - 1 + 127, 0) - down, 1)
    scale = np.exp2(byte - 127.0)
    codes = (blocks / scale).astype(np.float32).astype(dtype).astype(np.float64)
    return np.moveaxis((codes * scale).reshape(v.shape), -1, axis)


WIDE = False


def mx_kscale(k):
    if not WIDE:
        return np.ones(k)
    levels = np.array([10, -10, 5, -5, 0])
    if k % 512:
        return np.exp2(np.random.permutation(np.resize(levels, k // 32))).repeat(32)
    a = np.empty((k // 512, 16))
    for p in range(k // 512):
        a[p, :8] = np.random.permutation(np.resize(levels, 8))
        for g in range(8):
            far = levels[np.abs(levels - a[p, g]) >= 10]
            a[p, g + 8] = far[np.random.randint(len(far))]
    return np.exp2(a.ravel()).repeat(32)


def f64(x):
    return np.asarray(x).astype(np.float64)


def striped(idx):
    return np.tile(idx.reshape(-1, 16).T, (8, 1)).astype(np.uint16)


def unstriped(offs):
    return offs[:16].T.reshape(-1).astype(np.int64)


def pack_weight(w):
    k, n = w.shape
    w = f64(np.asarray(w, np.float32).astype(ml_dtypes.bfloat16)).reshape(k // 32, 32, n)
    amax = np.abs(w).max(1)
    byte = np.clip(np.where(amax > 0, np.frexp(amax)[1] - 1 + 127 - 7, 1), 1, 254)
    scaled = (w * np.exp2(127.0 - byte)[:, None, :]).reshape(k, n).astype(np.float32)
    words = np.ascontiguousarray(scaled.reshape(k // 512, 128, 4, n).transpose(0, 1, 3, 2)).astype(ml_dtypes.float8_e4m3fn).view(np.uint8)
    return words, np.ascontiguousarray(byte.astype(np.uint8).reshape(k // 512, 16, n))


def unpack_weight(words, scales):
    g, p, n, _ = words.shape
    vals = np.ascontiguousarray(words).view(ml_dtypes.float8_e4m3fn).astype(np.float64) * np.repeat(np.exp2(scales.astype(np.float64) - 127.0), 8, axis=1)[..., None]
    return vals.transpose(0, 1, 3, 2).reshape(g * 512, n)


def silu(v):
    return v / (1.0 + np.exp(-np.maximum(v, -700.0)))


K, T, S, H, N = 1024, 1024, 512, 512, 256
P = 2 ** 7


def setup_inputs():
    n = np.random.standard_normal
    s = mx_kscale(K)[:, None]
    u = mx_kscale(H)
    packed_xT = pack_weight(n((K, T)) * s)
    return {
        "x_words": packed_xT[0],
        "x_scales": packed_xT[1],
        "gate": np.tile(np.random.uniform(0.2, 1.0, S), (P, 1)).astype(np.float32),
        "res": n((N, T)).astype(np.float32),
        "w1": (n((K, H)) / np.sqrt(K) / s).astype(np.float32),
        "w3": (n((K, H)) / np.sqrt(K) / s * u).astype(np.float32),
        "w2": (n((H, N)) / np.sqrt(H) / u[:, None]).astype(np.float32),
        "offs": striped(np.random.permutation(T)[:S]),
    }


def reference(x_words, x_scales, gate, res, w1, w3, w2, offs):
    r = f64(res)[:, unstriped(offs)]
    xq = unpack_weight(x_words, x_scales)[:, unstriped(offs)]
    h = (silu(mxq(f64(w1), 0, "e4m3").T @ xq)) * ((mxq(f64(w3), 0, "e4m3").T @ xq))
    y = mxq(f64(w2), 0, "e4m3").T @ mxq(h, 0, "e4m3")
    out = f64(res).copy()
    out[:, unstriped(offs)] = r + y * f64(gate)[:1]
    return out

@@ -1,0 +1,191 @@
+from contextlib import ExitStack
+
+import concourse.mybir as mybir
+from concourse.masks import make_identity
+
+K, T, S, H, N = 1024, 1024, 512, 512, 256
+FLOPS = 2 * S * (2 * K * H + H * N)
+
+F32 = mybir.dt.float32
+BF16 = mybir.dt.bfloat16
+I32 = mybir.dt.int32
+U32 = mybir.dt.uint32
+U16 = mybir.dt.uint16
+U8 = mybir.dt.uint8
+FP8X4 = mybir.dt.float8_e4m3fn_x4
+ACT = mybir.ActivationFunctionType
+ALU = mybir.AluOpType
+
+P = 128
+PACK = 4
+K_PASS = P * PACK
+PASSES = K // K_PASS
+CHUNK = 128
+CHUNKS = S // CHUNK
+BLOCKS = N // P
+VEC_M = 80
+HALF = S // 2
+
+
+def tile_picked_modres_glusilu_p_kernel(
+    tc, x_words, x_scales, gate, res, w1, w3, w2, offs, out
+):
+    nc = tc.nc
+    with ExitStack() as ctx:
+        keep = ctx.enter_context(tc.tile_pool(name="keep", bufs=1))
+        psum = ctx.enter_context(tc.psum_pool(name="psum", bufs=1))
+
+        offsets = keep.tile([P, S // 16], U16, name="offsets")
+        nc.sync.dma_start(offsets[:], offs)
+
+        scale_table = keep.tile([P, T], U8, name="scale_table", align_bytes=64)
+        nc.vector.memset(scale_table[:].bitcast(I32), 0)
+        gate_rows = keep.tile([P, P], F32, name="gate_rows")
+        nc.gpsimd.memset(gate_rows[:], 0.0)
+        ident = keep.tile([P, P], F32, name="ident")
+        make_identity(nc, ident[:])
+        for q in range(4):
+            nc.scalar.dma_start(
+                scale_table[32 * q : 32 * q + 4 * PASSES, :].bitcast(I32),
+                x_scales[:, 4 * q : 4 * q + 4, :].bitcast(I32),
+            )
+        nc.scalar.dma_start(gate_rows[0:CHUNKS, :], gate[0].rearrange("(c p) -> c p", p=P))
+        warm = keep.tile([P, 1], F32, name="warm")
+        nc.scalar.activation(warm[:], ident[:, 0:1], ACT.Silu)
+
+        def load_words(g):
+            table = keep.tile([P, T], U32, name=f"word_table{g}", align_bytes=64)
+            nc.sync.dma_start(table[:].bitcast(I32), x_words[g].rearrange("p n t -> p (n t)").bitcast(I32))
+            return table
+
+        def load_rows(w, g, name):
+            raw = keep.tile([P, PACK, w.shape[1]], F32, name=name)
+            nc.sync.dma_start(raw[:], w[g * K_PASS : (g + 1) * K_PASS, :].rearrange("(p j) c -> p j c", j=PACK))
+            return raw
+
+        word_tables = [None] * PASSES
+        w1_raw = [None] * PASSES
+        for g in range(PASSES):
+            word_tables[g] = load_words(g)
+            w1_raw[g] = load_rows(w1, g, f"w1_raw{g}")
+        w3_raw = [load_rows(w3, g, f"w3_raw{g}") for g in range(PASSES)]
+        res_tiles = [keep.tile([P, T], F32, name=f"res{b}") for b in range(BLOCKS)]
+        nc.sync.dma_start(res_tiles[0][:], res[0:P, :])
+        w2_raw = load_rows(w2, 0, "w2_raw")
+        nc.sync.dma_start(res_tiles[1][:], res[P : 2 * P, :])
+
+        def quantize(grouped, width, name):
+            codes = keep.tile([P, width], U32, name=name + "_codes", align_bytes=64)
+            scales = keep.tile([P, width], U8, name=name + "_scales", align_bytes=64)
+            nc.vector.quantize_mx(out=codes[:].bitcast(FP8X4), scales=scales[:], in_=grouped)
+            return codes, scales
+
+        def quantize_first(raw, name):
+            grouped = keep.tile([P, H * PACK], BF16, name=name + "_bf16", align_bytes=64)
+            dst = grouped[:].rearrange("p (t m j) -> p m j t", t=PACK, j=PACK)
+            src = raw[:].rearrange("p j (m t) -> p m j t", t=PACK)
+            nc.vector.tensor_copy(dst[:, :VEC_M], src[:, :VEC_M])
+            nc.scalar.copy(dst[:, VEC_M:], src[:, VEC_M:])
+            return quantize(grouped[:], H, name)
+
+        x_codes = []
+        x_sc = keep.tile([P, S], U8, name="x_sc", align_bytes=64)
+        w1_q = []
+        for g in range(PASSES):
+            picked = keep.tile([P, S], U32, name=f"x_codes{g}", align_bytes=64)
+            nc.vector.tensor_copy(picked[:], word_tables[g][:].indirect(offsets[:]))
+            x_codes.append(picked)
+            if g == 0:
+                nc.vector.tensor_copy(x_sc[:], scale_table[:].indirect(offsets[:]))
+            w1_q.append(quantize_first(w1_raw[g], f"w1_{g}"))
+
+        gate_bank = psum.tile([P, P], F32, name="gate_bank", tag="up0")
+        nc.tensor.transpose(gate_bank[:], gate_rows[:], ident[:])
+        gate_col = keep.tile([P, CHUNKS], F32, name="gate_col")
+        nc.scalar.copy(gate_col[:], gate_bank[:, 0:CHUNKS])
+
+        def first_product(w_q, c, tag):
+            bank = psum.tile([P, PACK, CHUNK], F32, name=tag, tag=tag)
+            cols = slice(c * CHUNK, (c + 1) * CHUNK)
+            for t in range(PACK):
+                chans = slice(t * P, (t + 1) * P)
+                for g in range(PASSES):
+                    codes, scales = w_q[g]
+                    nc.tensor.matmul_mx(
+                        out=bank[:, t, :],
+                        lhsT=codes[:, chans].bitcast(FP8X4),
+                        lhsT_scale=scales[:, chans],
+                        rhs=x_codes[g][:, cols].bitcast(FP8X4),
+                        rhs_scale=x_sc[4 * g :, cols],
+                        start=(g == 0),
+                        stop=(g == PASSES - 1),
+                    )
+            return bank[:].rearrange("p t n -> p n t")
+
+        gates = []
+        for c in range(CHUNKS):
+            pre = first_product(w1_q, c, f"act{c}")
+            act = keep.tile([P, CHUNK, PACK], F32, name=f"silu{c}")
+            nc.scalar.activation(act[:], pre, ACT.Silu)
+            gates.append(act)
+
+        w3_q = [quantize_first(w3_raw[g], f"w3_{g}") for g in range(PASSES)]
+
+        old = [keep.tile([P, S], F32, name=f"old{b}") for b in range(BLOCKS)]
+        nc.vector.tensor_copy(old[0][:], res_tiles[0][:].indirect(offsets[:]))
+
+        w2_bf16 = keep.tile([P, N * PACK], BF16, name="w2_bf16", align_bytes=64)
+        nc.scalar.copy(
+            w2_bf16[:].rearrange("p (c i j) -> p c j i", i=4, j=PACK),
+            w2_raw[:].rearrange("p j (c i) -> p c j i", i=4),
+        )
+
+        w2_q = []
+        gated = [keep.tile([P, BLOCKS, HALF], F32, name=f"gated{half}") for half in range(2)]
+
+        def hidden(c):
+            up = first_product(w3_q, c, f"up{c}")
+            h = keep.tile([P, CHUNK, PACK], BF16, name=f"h{c}", align_bytes=64)
+            nc.vector.tensor_tensor(h[:], up, gates[c][:], ALU.mult)
+            return h
+
+        def second_product(c, h):
+            h_codes, h_scales = quantize(h[:].rearrange("p n t -> p (n t)"), CHUNK, f"h{c}")
+            w2_codes, w2_scales = w2_q[0]
+            bank = psum.tile([P, 2, N], F32, name=f"down{c}", tag=f"act{c}")
+            nc.tensor.matmul_mx(
+                out=bank[:, 0, :],
+                lhsT=h_codes[:].bitcast(FP8X4),
+                lhsT_scale=h_scales[:],
+                rhs=w2_codes[:].bitcast(FP8X4),
+                rhs_scale=w2_scales[:],
+                start=True,
+                stop=True,
+            )
+            y_rows = keep.tile([P, N], F32, name=f"y_rows{c}")
+            nc.scalar.activation(y_rows[:], bank[:, 0, :], ACT.Copy, scale=gate_col[:, c : c + 1])
+            for b in range(BLOCKS):
+                nc.tensor.transpose(bank[:, 1, b * P : (b + 1) * P], y_rows[:, b * P : (b + 1) * P], ident[:])
+            half, at = divmod(c * CHUNK, HALF)
+            nc.scalar.copy(
+                gated[half][:, :, at : at + CHUNK],
+                bank[:, 1, :].rearrange("p (b n) -> p b n", b=BLOCKS),
+            )
+
+        h_bf16 = []
+        for c in range(CHUNKS):
+            h_bf16.append(hidden(c))
+            if c == 0:
+                w2_q.append(quantize(w2_bf16[:], N, "w2"))
+            else:
+                second_product(c - 1, h_bf16[c - 1])
+        nc.vector.tensor_copy(old[1][:], res_tiles[1][:].indirect(offsets[:]))
+        second_product(CHUNKS - 1, h_bf16[CHUNKS - 1])
+
+        for half in range(2):
+            cols = slice(half * HALF, (half + 1) * HALF)
+            entries = offsets[:, half * HALF // 16 : (half + 1) * HALF // 16]
+            for b in range(BLOCKS):
+                nc.vector.tensor_tensor(res_tiles[b][:].indirect(entries), old[b][:, cols], gated[half][:, b, :], ALU.add)
+        for b in range(BLOCKS):
+            nc.sync.dma_start(out[b * P : (b + 1) * P, :], res_tiles[b][:])

@@ -23,7 +23,7 @@ PASSES = K // K_PASS
 CHUNK = 128
 CHUNKS = S // CHUNK
 BLOCKS = N // P
-VEC_M = 80
+VEC_M = 88
 HALF = S // 2
 
 
@@ -59,15 +59,13 @@ def tile_picked_modres_glusilu_p_kernel(
             return table
 
         def load_rows(w, g, name):
-            raw = keep.tile([P, PACK, w.shape[1]], F32, name=name)
+            raw = keep.tile([P, PACK, w.shape[1]], F32, name=name, tag=name)
             nc.sync.dma_start(raw[:], w[g * K_PASS : (g + 1) * K_PASS, :].rearrange("(p j) c -> p j c", j=PACK))
             return raw
 
-        word_tables = [None] * PASSES
-        w1_raw = [None] * PASSES
-        for g in range(PASSES):
-            word_tables[g] = load_words(g)
-            w1_raw[g] = load_rows(w1, g, f"w1_raw{g}")
+        word_tables = [load_words(0)]
+        w1_raw = [load_rows(w1, g, f"w1_raw{g}") for g in range(PASSES)]
+        word_tables.append(load_words(1))
         w3_raw = [load_rows(w3, g, f"w3_raw{g}") for g in range(PASSES)]
         res_tiles = [keep.tile([P, T], F32, name=f"res{b}") for b in range(BLOCKS)]
         nc.sync.dma_start(res_tiles[0][:], res[0:P, :])
@@ -81,7 +79,7 @@ def tile_picked_modres_glusilu_p_kernel(
             return codes, scales
 
         def quantize_first(raw, name):
-            grouped = keep.tile([P, H * PACK], BF16, name=name + "_bf16", align_bytes=64)
+            grouped = keep.tile([P, H * PACK], BF16, name=name + "_bf16", tag=name + "_bf16", align_bytes=64)
             dst = grouped[:].rearrange("p (t m j) -> p m j t", t=PACK, j=PACK)
             src = raw[:].rearrange("p j (m t) -> p m j t", t=PACK)
             nc.vector.tensor_copy(dst[:, :VEC_M], src[:, :VEC_M])
@@ -93,11 +91,17 @@ def tile_picked_modres_glusilu_p_kernel(
         w1_q = []
         for g in range(PASSES):
             picked = keep.tile([P, S], U32, name=f"x_codes{g}", align_bytes=64)
-            nc.vector.tensor_copy(picked[:], word_tables[g][:].indirect(offsets[:]))
             x_codes.append(picked)
-            if g == 0:
-                nc.vector.tensor_copy(x_sc[:], scale_table[:].indirect(offsets[:]))
             w1_q.append(quantize_first(w1_raw[g], f"w1_{g}"))
+        nc.vector.tensor_copy(x_codes[0][:], word_tables[0][:].indirect(offsets[:]))
+        nc.vector.tensor_copy(x_sc[:], scale_table[:].indirect(offsets[:]))
+        for c in range(CHUNKS):
+            nc.vector.tensor_copy(
+                x_codes[1][:, c * CHUNK : (c + 1) * CHUNK],
+                word_tables[1][:].indirect(offsets[:, c * CHUNK // 16 : (c + 1) * CHUNK // 16]),
+            )
+
+        w3_q = [quantize_first(w3_raw[g], f"w3_{g}") for g in range(PASSES)]
 
         gate_bank = psum.tile([P, P], F32, name="gate_bank", tag="up0")
         nc.tensor.transpose(gate_bank[:], gate_rows[:], ident[:])
@@ -122,21 +126,23 @@ def tile_picked_modres_glusilu_p_kernel(
                     )
             return bank[:].rearrange("p t n -> p n t")
 
+        early = keep.tile([P, S // 2 * PACK], F32, name="silu_early", tag="w3_raw0")
+        later = keep.tile([P, S // 2 * PACK], F32, name="silu_later", tag="w3_raw1")
         gates = []
         for c in range(CHUNKS):
             pre = first_product(w1_q, c, f"act{c}")
-            act = keep.tile([P, CHUNK, PACK], F32, name=f"silu{c}")
-            nc.scalar.activation(act[:], pre, ACT.Silu)
+            at = c % 2 * CHUNK * PACK
+            act = (early if c < 2 else later)[:, at : at + CHUNK * PACK].rearrange("p (n t) -> p n t", t=PACK)
+            nc.scalar.activation(act, pre, ACT.Silu)
             gates.append(act)
 
-        w3_q = [quantize_first(w3_raw[g], f"w3_{g}") for g in range(PASSES)]
+        late = keep.tile([P, 2 * S], F32, name="late", tag="w3_1_bf16", align_bytes=64)
+        old = [late[:, :S]]
+        nc.vector.tensor_copy(old[0], res_tiles[0][:].indirect(offsets[:]))
 
-        old = [keep.tile([P, S], F32, name=f"old{b}") for b in range(BLOCKS)]
-        nc.vector.tensor_copy(old[0][:], res_tiles[0][:].indirect(offsets[:]))
-
-        w2_bf16 = keep.tile([P, N * PACK], BF16, name="w2_bf16", align_bytes=64)
+        w2_bf16 = late[:, S:].bitcast(BF16)
         nc.scalar.copy(
-            w2_bf16[:].rearrange("p (c i j) -> p c j i", i=4, j=PACK),
+            w2_bf16.rearrange("p (c i j) -> p c j i", i=4, j=PACK),
             w2_raw[:].rearrange("p j (c i) -> p c j i", i=4),
         )
 
@@ -145,8 +151,8 @@ def tile_picked_modres_glusilu_p_kernel(
 
         def hidden(c):
             up = first_product(w3_q, c, f"up{c}")
-            h = keep.tile([P, CHUNK, PACK], BF16, name=f"h{c}", align_bytes=64)
-            nc.vector.tensor_tensor(h[:], up, gates[c][:], ALU.mult)
+            h = keep.tile([P, CHUNK, PACK], BF16, name=f"h{c}", tag=f"h{c}", align_bytes=64)
+            nc.vector.tensor_tensor(h[:], up, gates[c], ALU.mult)
             return h
 
         def second_product(c, h):
@@ -176,11 +182,13 @@ def tile_picked_modres_glusilu_p_kernel(
         for c in range(CHUNKS):
             h_bf16.append(hidden(c))
             if c == 0:
-                w2_q.append(quantize(w2_bf16[:], N, "w2"))
+                w2_q.append(quantize(w2_bf16, N, "w2"))
             else:
                 second_product(c - 1, h_bf16[c - 1])
-        nc.vector.tensor_copy(old[1][:], res_tiles[1][:].indirect(offsets[:]))
         second_product(CHUNKS - 1, h_bf16[CHUNKS - 1])
+        old1 = keep.tile([P, S], F32, name="old1", tag=f"h{CHUNKS - 1}", align_bytes=64)
+        old.append(old1[:])
+        nc.vector.tensor_copy(old[1], res_tiles[1][:].indirect(offsets[:]))
 
         for half in range(2):
             cols = slice(half * HALF, (half + 1) * HALF)

@@ -23,7 +23,7 @@ PASSES = K // K_PASS
 CHUNK = 128
 CHUNKS = S // CHUNK
 BLOCKS = N // P
-VEC_M = 88
+VEC_M = 84
 HALF = S // 2
 
 
@@ -59,7 +59,7 @@ def tile_picked_modres_glusilu_p_kernel(
             return table
 
         def load_rows(w, g, name):
-            raw = keep.tile([P, PACK, w.shape[1]], F32, name=name, tag=name)
+            raw = keep.tile([P, PACK, w.shape[1]], F32, name=name, tag=name, align_bytes=64)
             nc.sync.dma_start(raw[:], w[g * K_PASS : (g + 1) * K_PASS, :].rearrange("(p j) c -> p j c", j=PACK))
             return raw
 
@@ -126,8 +126,9 @@ def tile_picked_modres_glusilu_p_kernel(
                     )
             return bank[:].rearrange("p t n -> p n t")
 
-        early = keep.tile([P, S // 2 * PACK], F32, name="silu_early", tag="w3_raw0")
-        later = keep.tile([P, S // 2 * PACK], F32, name="silu_later", tag="w3_raw1")
+        early = keep.tile([P, S // 2 * PACK], F32, name="silu_early", tag="w3_raw0", align_bytes=64)
+        late = keep.tile([P, PACK * H], F32, name="late", tag="w3_raw1", align_bytes=64)
+        later = late[:, : S // 2 * PACK]
         gates = []
         for c in range(CHUNKS):
             pre = first_product(w1_q, c, f"act{c}")
@@ -136,11 +137,10 @@ def tile_picked_modres_glusilu_p_kernel(
             nc.scalar.activation(act, pre, ACT.Silu)
             gates.append(act)
 
-        late = keep.tile([P, 2 * S], F32, name="late", tag="w3_1_bf16", align_bytes=64)
-        old = [late[:, :S]]
+        old = [late[:, 2 * S : 3 * S]]
         nc.vector.tensor_copy(old[0], res_tiles[0][:].indirect(offsets[:]))
 
-        w2_bf16 = late[:, S:].bitcast(BF16)
+        w2_bf16 = late[:, 3 * S :].bitcast(BF16)
         nc.scalar.copy(
             w2_bf16.rearrange("p (c i j) -> p c j i", i=4, j=PACK),
             w2_raw[:].rearrange("p j (c i) -> p c j i", i=4),
@@ -151,7 +151,7 @@ def tile_picked_modres_glusilu_p_kernel(
 
         def hidden(c):
             up = first_product(w3_q, c, f"up{c}")
-            h = keep.tile([P, CHUNK, PACK], BF16, name=f"h{c}", tag=f"h{c}", align_bytes=64)
+            h = keep.tile([P, CHUNK, PACK], BF16, name=f"h{c}", tag="w2_raw" if c == 2 else f"h{c}", align_bytes=64)
             nc.vector.tensor_tensor(h[:], up, gates[c], ALU.mult)
             return h
 
@@ -185,9 +185,9 @@ def tile_picked_modres_glusilu_p_kernel(
                 w2_q.append(quantize(w2_bf16, N, "w2"))
             else:
                 second_product(c - 1, h_bf16[c - 1])
-        second_product(CHUNKS - 1, h_bf16[CHUNKS - 1])
-        old1 = keep.tile([P, S], F32, name="old1", tag=f"h{CHUNKS - 1}", align_bytes=64)
+        old1 = keep.tile([P, S], F32, name="old1", tag="w2_raw", align_bytes=64)
         old.append(old1[:])
+        second_product(CHUNKS - 1, h_bf16[CHUNKS - 1])
         nc.vector.tensor_copy(old[1], res_tiles[1][:].indirect(offsets[:]))
 
         for half in range(2):

@@ -23,8 +23,8 @@ PASSES = K // K_PASS
 CHUNK = 128
 CHUNKS = S // CHUNK
 BLOCKS = N // P
-VEC_M = 84
-HALF = S // 2
+VEC_M = 80
+PIECES = ((0, CHUNK), (CHUNK, 2 * CHUNK), (2 * CHUNK, S))
 
 
 def tile_picked_modres_glusilu_p_kernel(
@@ -147,7 +147,7 @@ def tile_picked_modres_glusilu_p_kernel(
         )
 
         w2_q = []
-        gated = [keep.tile([P, BLOCKS, HALF], F32, name=f"gated{half}") for half in range(2)]
+        gated = [keep.tile([P, BLOCKS, last - first], F32, name=f"gated{first}") for first, last in PIECES]
 
         def hidden(c):
             up = first_product(w3_q, c, f"up{c}")
@@ -172,9 +172,10 @@ def tile_picked_modres_glusilu_p_kernel(
             nc.scalar.activation(y_rows[:], bank[:, 0, :], ACT.Copy, scale=gate_col[:, c : c + 1])
             for b in range(BLOCKS):
                 nc.tensor.transpose(bank[:, 1, b * P : (b + 1) * P], y_rows[:, b * P : (b + 1) * P], ident[:])
-            half, at = divmod(c * CHUNK, HALF)
+            piece = min(c, len(PIECES) - 1)
+            at = c * CHUNK - PIECES[piece][0]
             nc.scalar.copy(
-                gated[half][:, :, at : at + CHUNK],
+                gated[piece][:, :, at : at + CHUNK],
                 bank[:, 1, :].rearrange("p (b n) -> p b n", b=BLOCKS),
             )
 
@@ -185,15 +186,15 @@ def tile_picked_modres_glusilu_p_kernel(
                 w2_q.append(quantize(w2_bf16, N, "w2"))
             else:
                 second_product(c - 1, h_bf16[c - 1])
-        old1 = keep.tile([P, S], F32, name="old1", tag="w2_raw", align_bytes=64)
-        old.append(old1[:])
-        second_product(CHUNKS - 1, h_bf16[CHUNKS - 1])
+        old.append(late[:, 3 * S :])
         nc.vector.tensor_copy(old[1], res_tiles[1][:].indirect(offsets[:]))
+        second_product(CHUNKS - 1, h_bf16[CHUNKS - 1])
 
-        for half in range(2):
-            cols = slice(half * HALF, (half + 1) * HALF)
-            entries = offsets[:, half * HALF // 16 : (half + 1) * HALF // 16]
+        for piece, (first, last) in enumerate(PIECES):
+            entries = offsets[:, first // 16 : last // 16]
             for b in range(BLOCKS):
-                nc.vector.tensor_tensor(res_tiles[b][:].indirect(entries), old[b][:, cols], gated[half][:, b, :], ALU.add)
+                nc.vector.tensor_tensor(
+                    res_tiles[b][:].indirect(entries), old[b][:, first:last], gated[piece][:, b, :], ALU.add
+                )
         for b in range(BLOCKS):
             nc.sync.dma_start(out[b * P : (b + 1) * P, :], res_tiles[b][:])

@@ -24,6 +24,7 @@ CHUNK = 128
 CHUNKS = S // CHUNK
 BLOCKS = N // P
 VEC_M = 80
+VEC_M_BUSY = 92
 PIECES = ((0, CHUNK), (CHUNK, 2 * CHUNK), (2 * CHUNK, S))
 
 
@@ -78,12 +79,12 @@ def tile_picked_modres_glusilu_p_kernel(
             nc.vector.quantize_mx(out=codes[:].bitcast(FP8X4), scales=scales[:], in_=grouped)
             return codes, scales
 
-        def quantize_first(raw, name):
+        def quantize_first(raw, name, on_vector):
             grouped = keep.tile([P, H * PACK], BF16, name=name + "_bf16", tag=name + "_bf16", align_bytes=64)
             dst = grouped[:].rearrange("p (t m j) -> p m j t", t=PACK, j=PACK)
             src = raw[:].rearrange("p j (m t) -> p m j t", t=PACK)
-            nc.vector.tensor_copy(dst[:, :VEC_M], src[:, :VEC_M])
-            nc.scalar.copy(dst[:, VEC_M:], src[:, VEC_M:])
+            nc.vector.tensor_copy(dst[:, :on_vector], src[:, :on_vector])
+            nc.scalar.copy(dst[:, on_vector:], src[:, on_vector:])
             return quantize(grouped[:], H, name)
 
         x_codes = []
@@ -92,7 +93,7 @@ def tile_picked_modres_glusilu_p_kernel(
         for g in range(PASSES):
             picked = keep.tile([P, S], U32, name=f"x_codes{g}", align_bytes=64)
             x_codes.append(picked)
-            w1_q.append(quantize_first(w1_raw[g], f"w1_{g}"))
+            w1_q.append(quantize_first(w1_raw[g], f"w1_{g}", VEC_M))
         nc.vector.tensor_copy(x_codes[0][:], word_tables[0][:].indirect(offsets[:]))
         nc.vector.tensor_copy(x_sc[:], scale_table[:].indirect(offsets[:]))
         for c in range(CHUNKS):
@@ -101,7 +102,7 @@ def tile_picked_modres_glusilu_p_kernel(
                 word_tables[1][:].indirect(offsets[:, c * CHUNK // 16 : (c + 1) * CHUNK // 16]),
             )
 
-        w3_q = [quantize_first(w3_raw[g], f"w3_{g}") for g in range(PASSES)]
+        w3_q = [quantize_first(w3_raw[g], f"w3_{g}", (VEC_M_BUSY, VEC_M)[g]) for g in range(PASSES)]
 
         gate_bank = psum.tile([P, P], F32, name="gate_bank", tag="up0")
         nc.tensor.transpose(gate_bank[:], gate_rows[:], ident[:])
@@ -131,7 +132,7 @@ def tile_picked_modres_glusilu_p_kernel(
         later = late[:, : S // 2 * PACK]
         gates = []
         for c in range(CHUNKS):
-            pre = first_product(w1_q, c, f"act{c}")
+            pre = first_product(w1_q, c, f"act{c % 2}")
             at = c % 2 * CHUNK * PACK
             act = (early if c < 2 else later)[:, at : at + CHUNK * PACK].rearrange("p (n t) -> p n t", t=PACK)
             nc.scalar.activation(act, pre, ACT.Silu)

@@ -24,7 +24,7 @@ CHUNK = 128
 CHUNKS = S // CHUNK
 BLOCKS = N // P
 VEC_M = 80
-VEC_M_BUSY = 92
+VEC_M_BUSY = 84
 PIECES = ((0, CHUNK), (CHUNK, 2 * CHUNK), (2 * CHUNK, S))
 
 
@@ -67,10 +67,11 @@ def tile_picked_modres_glusilu_p_kernel(
         word_tables = [load_words(0)]
         w1_raw = [load_rows(w1, g, f"w1_raw{g}") for g in range(PASSES)]
         word_tables.append(load_words(1))
-        w3_raw = [load_rows(w3, g, f"w3_raw{g}") for g in range(PASSES)]
+        w3_raw = [load_rows(w3, 0, "w3_raw0")]
+        w3_halves = [load_rows(w3[:, u * H // 2 : (u + 1) * H // 2], 1, f"w3_half{u}") for u in range(2)]
         res_tiles = [keep.tile([P, T], F32, name=f"res{b}") for b in range(BLOCKS)]
         nc.sync.dma_start(res_tiles[0][:], res[0:P, :])
-        w2_raw = load_rows(w2, 0, "w2_raw")
+        w2_raw = [load_rows(w2[:, b * P : (b + 1) * P], 0, f"w2_raw{b}") for b in range(BLOCKS)]
         nc.sync.dma_start(res_tiles[1][:], res[P : 2 * P, :])
 
         def quantize(grouped, width, name):
@@ -102,33 +103,42 @@ def tile_picked_modres_glusilu_p_kernel(
                 word_tables[1][:].indirect(offsets[:, c * CHUNK // 16 : (c + 1) * CHUNK // 16]),
             )
 
-        w3_q = [quantize_first(w3_raw[g], f"w3_{g}", (VEC_M_BUSY, VEC_M)[g]) for g in range(PASSES)]
+        w3_q = [quantize_first(w3_raw[0], "w3_0", VEC_M_BUSY)]
+        grouped = keep.tile([P, H * PACK], BF16, name="w3_1_bf16", align_bytes=64)
+        dst = grouped[:].rearrange("p (t m j) -> p m j t", t=PACK, j=PACK)
+        src = [half[:].rearrange("p j (m t) -> p m j t", t=PACK) for half in w3_halves]
+        nc.vector.tensor_copy(dst[:, : P // 2], src[0])
+        nc.vector.tensor_copy(dst[:, P // 2 : P // 2 + VEC_M // 2], src[1][:, : VEC_M // 2])
+        nc.scalar.copy(dst[:, P // 2 + VEC_M // 2 :], src[1][:, VEC_M // 2 :])
+        w3_q.append(quantize(grouped[:], H, "w3_1"))
 
         gate_bank = psum.tile([P, P], F32, name="gate_bank", tag="up0")
         nc.tensor.transpose(gate_bank[:], gate_rows[:], ident[:])
         gate_col = keep.tile([P, CHUNKS], F32, name="gate_col")
         nc.scalar.copy(gate_col[:], gate_bank[:, 0:CHUNKS])
 
-        def first_product(w_q, c, tag):
+        def first_product(w_q, c, tag, by_pass=False):
             bank = psum.tile([P, PACK, CHUNK], F32, name=tag, tag=tag)
             cols = slice(c * CHUNK, (c + 1) * CHUNK)
-            for t in range(PACK):
+            steps = [(t, g) for t in range(PACK) for g in range(PASSES)]
+            if by_pass:
+                steps = [(t, g) for g in range(PASSES) for t in range(PACK)]
+            for t, g in steps:
                 chans = slice(t * P, (t + 1) * P)
-                for g in range(PASSES):
-                    codes, scales = w_q[g]
-                    nc.tensor.matmul_mx(
-                        out=bank[:, t, :],
-                        lhsT=codes[:, chans].bitcast(FP8X4),
-                        lhsT_scale=scales[:, chans],
-                        rhs=x_codes[g][:, cols].bitcast(FP8X4),
-                        rhs_scale=x_sc[4 * g :, cols],
-                        start=(g == 0),
-                        stop=(g == PASSES - 1),
-                    )
+                codes, scales = w_q[g]
+                nc.tensor.matmul_mx(
+                    out=bank[:, t, :],
+                    lhsT=codes[:, chans].bitcast(FP8X4),
+                    lhsT_scale=scales[:, chans],
+                    rhs=x_codes[g][:, cols].bitcast(FP8X4),
+                    rhs_scale=x_sc[4 * g :, cols],
+                    start=(t, g) == steps[0] if by_pass else g == 0,
+                    stop=(t, g) == steps[-1] if by_pass else g == PASSES - 1,
+                )
             return bank[:].rearrange("p t n -> p n t")
 
         early = keep.tile([P, S // 2 * PACK], F32, name="silu_early", tag="w3_raw0", align_bytes=64)
-        late = keep.tile([P, PACK * H], F32, name="late", tag="w3_raw1", align_bytes=64)
+        late = keep.tile([P, PACK * H], F32, name="late", tag="w3_half1", align_bytes=64)
         later = late[:, : S // 2 * PACK]
         gates = []
         for c in range(CHUNKS):
@@ -142,17 +152,18 @@ def tile_picked_modres_glusilu_p_kernel(
         nc.vector.tensor_copy(old[0], res_tiles[0][:].indirect(offsets[:]))
 
         w2_bf16 = late[:, 3 * S :].bitcast(BF16)
-        nc.scalar.copy(
-            w2_bf16.rearrange("p (c i j) -> p c j i", i=4, j=PACK),
-            w2_raw[:].rearrange("p j (c i) -> p c j i", i=4),
-        )
+        for b in range(BLOCKS):
+            nc.scalar.copy(
+                w2_bf16[:, b * P * PACK : (b + 1) * P * PACK].rearrange("p (c i j) -> p c j i", i=4, j=PACK),
+                w2_raw[b][:].rearrange("p j (c i) -> p c j i", i=4),
+            )
 
         w2_q = []
         gated = [keep.tile([P, BLOCKS, last - first], F32, name=f"gated{first}") for first, last in PIECES]
 
         def hidden(c):
-            up = first_product(w3_q, c, f"up{c}")
-            h = keep.tile([P, CHUNK, PACK], BF16, name=f"h{c}", tag="w2_raw" if c == 2 else f"h{c}", align_bytes=64)
+            up = first_product(w3_q, c, f"up{c}", by_pass=c >= 2)
+            h = keep.tile([P, CHUNK, PACK], BF16, name=f"h{c}", tag="w2_raw1" if c == 2 else f"h{c}", align_bytes=64)
             nc.vector.tensor_tensor(h[:], up, gates[c], ALU.mult)
             return h
 

@@ -24,6 +24,7 @@ CHUNK = 128
 CHUNKS = S // CHUNK
 BLOCKS = N // P
 VEC_M = 80
+VEC_M_FIRST = 36
 VEC_M_BUSY = 84
 PIECES = ((0, CHUNK), (CHUNK, 2 * CHUNK), (2 * CHUNK, S))
 
@@ -45,28 +46,24 @@ def tile_picked_modres_glusilu_p_kernel(
         nc.gpsimd.memset(gate_rows[:], 0.0)
         ident = keep.tile([P, P], F32, name="ident")
         make_identity(nc, ident[:])
-        for q in range(4):
-            nc.scalar.dma_start(
-                scale_table[32 * q : 32 * q + 4 * PASSES, :].bitcast(I32),
-                x_scales[:, 4 * q : 4 * q + 4, :].bitcast(I32),
-            )
         nc.scalar.dma_start(gate_rows[0:CHUNKS, :], gate[0].rearrange("(c p) -> c p", p=P))
         warm = keep.tile([P, 1], F32, name="warm")
         nc.scalar.activation(warm[:], ident[:, 0:1], ACT.Silu)
 
-        def load_words(g):
-            table = keep.tile([P, T], U32, name=f"word_table{g}", align_bytes=64)
-            nc.sync.dma_start(table[:].bitcast(I32), x_words[g].rearrange("p n t -> p (n t)").bitcast(I32))
-            return table
+        word_table = keep.tile([P, PASSES, T], U32, name="word_table", align_bytes=64)
+        nc.sync.dma_start(word_table[:].bitcast(I32), x_words.rearrange("g p n t -> p g (n t)").bitcast(I32))
+        for q in range(4):
+            nc.sync.dma_start(
+                scale_table[32 * q : 32 * q + 4 * PASSES, :].bitcast(I32),
+                x_scales[:, 4 * q : 4 * q + 4, :].bitcast(I32),
+            )
 
         def load_rows(w, g, name):
             raw = keep.tile([P, PACK, w.shape[1]], F32, name=name, tag=name, align_bytes=64)
             nc.sync.dma_start(raw[:], w[g * K_PASS : (g + 1) * K_PASS, :].rearrange("(p j) c -> p j c", j=PACK))
             return raw
 
-        word_tables = [load_words(0)]
         w1_raw = [load_rows(w1, g, f"w1_raw{g}") for g in range(PASSES)]
-        word_tables.append(load_words(1))
         w3_raw = [load_rows(w3, 0, "w3_raw0")]
         w3_halves = [load_rows(w3[:, u * H // 2 : (u + 1) * H // 2], 1, f"w3_half{u}") for u in range(2)]
         res_tiles = [keep.tile([P, T], F32, name=f"res{b}") for b in range(BLOCKS)]
@@ -88,20 +85,12 @@ def tile_picked_modres_glusilu_p_kernel(
             nc.scalar.copy(dst[:, on_vector:], src[:, on_vector:])
             return quantize(grouped[:], H, name)
 
-        x_codes = []
-        x_sc = keep.tile([P, S], U8, name="x_sc", align_bytes=64)
-        w1_q = []
+        x_codes = [keep.tile([P, S], U32, name=f"x_codes{g}", align_bytes=64) for g in range(PASSES)]
         for g in range(PASSES):
-            picked = keep.tile([P, S], U32, name=f"x_codes{g}", align_bytes=64)
-            x_codes.append(picked)
-            w1_q.append(quantize_first(w1_raw[g], f"w1_{g}", VEC_M))
-        nc.vector.tensor_copy(x_codes[0][:], word_tables[0][:].indirect(offsets[:]))
+            nc.vector.tensor_copy(x_codes[g][:], word_table[:, g, :].indirect(offsets[:]))
+        x_sc = keep.tile([P, S], U8, name="x_sc", align_bytes=64)
         nc.vector.tensor_copy(x_sc[:], scale_table[:].indirect(offsets[:]))
-        for c in range(CHUNKS):
-            nc.vector.tensor_copy(
-                x_codes[1][:, c * CHUNK : (c + 1) * CHUNK],
-                word_tables[1][:].indirect(offsets[:, c * CHUNK // 16 : (c + 1) * CHUNK // 16]),
-            )
+        w1_q = [quantize_first(w1_raw[g], f"w1_{g}", (VEC_M_FIRST, VEC_M)[g]) for g in range(PASSES)]
 
         w3_q = [quantize_first(w3_raw[0], "w3_0", VEC_M_BUSY)]
         grouped = keep.tile([P, H * PACK], BF16, name="w3_1_bf16", align_bytes=64)
@@ -112,7 +101,7 @@ def tile_picked_modres_glusilu_p_kernel(
         nc.scalar.copy(dst[:, P // 2 + VEC_M // 2 :], src[1][:, VEC_M // 2 :])
         w3_q.append(quantize(grouped[:], H, "w3_1"))
 
-        gate_bank = psum.tile([P, P], F32, name="gate_bank", tag="up0")
+        gate_bank = psum.tile([P, P], F32, name="gate_bank", tag="act3")
         nc.tensor.transpose(gate_bank[:], gate_rows[:], ident[:])
         gate_col = keep.tile([P, CHUNKS], F32, name="gate_col")
         nc.scalar.copy(gate_col[:], gate_bank[:, 0:CHUNKS])
@@ -142,7 +131,7 @@ def tile_picked_modres_glusilu_p_kernel(
         later = late[:, : S // 2 * PACK]
         gates = []
         for c in range(CHUNKS):
-            pre = first_product(w1_q, c, f"act{c % 2}")
+            pre = first_product(w1_q, c, f"act{c % 2}", by_pass=True)
             at = c % 2 * CHUNK * PACK
             act = (early if c < 2 else later)[:, at : at + CHUNK * PACK].rearrange("p (n t) -> p n t", t=PACK)
             nc.scalar.activation(act, pre, ACT.Silu)

@@ -38,7 +38,6 @@ def tile_picked_modres_glusilu_p_kernel(
         psum = ctx.enter_context(tc.psum_pool(name="psum", bufs=1))
 
         offsets = keep.tile([P, S // 16], U16, name="offsets")
-        nc.sync.dma_start(offsets[:], offs)
 
         scale_table = keep.tile([P, T], U8, name="scale_table", align_bytes=64)
         nc.vector.memset(scale_table[:].bitcast(I32), 0)
@@ -46,17 +45,19 @@ def tile_picked_modres_glusilu_p_kernel(
         nc.gpsimd.memset(gate_rows[:], 0.0)
         ident = keep.tile([P, P], F32, name="ident")
         make_identity(nc, ident[:])
-        nc.scalar.dma_start(gate_rows[0:CHUNKS, :], gate[0].rearrange("(c p) -> c p", p=P))
         warm = keep.tile([P, 1], F32, name="warm")
         nc.scalar.activation(warm[:], ident[:, 0:1], ACT.Silu)
 
         word_table = keep.tile([P, PASSES, T], U32, name="word_table", align_bytes=64)
         nc.sync.dma_start(word_table[:].bitcast(I32), x_words.rearrange("g p n t -> p g (n t)").bitcast(I32))
+        nc.sync.dma_start(offsets[:], offs)
         for q in range(4):
             nc.sync.dma_start(
                 scale_table[32 * q : 32 * q + 4 * PASSES, :].bitcast(I32),
                 x_scales[:, 4 * q : 4 * q + 4, :].bitcast(I32),
             )
+
+        nc.sync.dma_start(gate_rows[0:CHUNKS, :], gate[0].rearrange("(c p) -> c p", p=P))
 
         def load_rows(w, g, name):
             raw = keep.tile([P, PACK, w.shape[1]], F32, name=name, tag=name, align_bytes=64)

@@ -24,7 +24,7 @@ CHUNK = 128
 CHUNKS = S // CHUNK
 BLOCKS = N // P
 VEC_M = 80
-VEC_M_FIRST = 36
+VEC_M_FIRST = 72
 VEC_M_BUSY = 84
 PIECES = ((0, CHUNK), (CHUNK, 2 * CHUNK), (2 * CHUNK, S))
 
@@ -48,16 +48,20 @@ def tile_picked_modres_glusilu_p_kernel(
         warm = keep.tile([P, 1], F32, name="warm")
         nc.scalar.activation(warm[:], ident[:, 0:1], ACT.Silu)
 
-        word_table = keep.tile([P, PASSES, T], U32, name="word_table", align_bytes=64)
-        nc.sync.dma_start(word_table[:].bitcast(I32), x_words.rearrange("g p n t -> p g (n t)").bitcast(I32))
+        word_tables = [keep.tile([P, T], U32, name=f"word_table{g}", align_bytes=64) for g in range(PASSES)]
+
+        def load_words(g):
+            nc.sync.dma_start(word_tables[g][:].bitcast(I32), x_words[g].rearrange("p n t -> p (n t)").bitcast(I32))
+
+        load_words(0)
         nc.sync.dma_start(offsets[:], offs)
+        load_words(1)
         for q in range(4):
             nc.sync.dma_start(
                 scale_table[32 * q : 32 * q + 4 * PASSES, :].bitcast(I32),
                 x_scales[:, 4 * q : 4 * q + 4, :].bitcast(I32),
             )
 
-        nc.sync.dma_start(gate_rows[0:CHUNKS, :], gate[0].rearrange("(c p) -> c p", p=P))
 
         def load_rows(w, g, name):
             raw = keep.tile([P, PACK, w.shape[1]], F32, name=name, tag=name, align_bytes=64)
@@ -65,6 +69,7 @@ def tile_picked_modres_glusilu_p_kernel(
             return raw
 
         w1_raw = [load_rows(w1, g, f"w1_raw{g}") for g in range(PASSES)]
+        nc.sync.dma_start(gate_rows[0:CHUNKS, :], gate[0].rearrange("(c p) -> c p", p=P))
         w3_raw = [load_rows(w3, 0, "w3_raw0")]
         w3_halves = [load_rows(w3[:, u * H // 2 : (u + 1) * H // 2], 1, f"w3_half{u}") for u in range(2)]
         res_tiles = [keep.tile([P, T], F32, name=f"res{b}") for b in range(BLOCKS)]
@@ -88,7 +93,7 @@ def tile_picked_modres_glusilu_p_kernel(
 
         x_codes = [keep.tile([P, S], U32, name=f"x_codes{g}", align_bytes=64) for g in range(PASSES)]
         for g in range(PASSES):
-            nc.vector.tensor_copy(x_codes[g][:], word_table[:, g, :].indirect(offsets[:]))
+            nc.vector.tensor_copy(x_codes[g][:], word_tables[g][:].indirect(offsets[:]))
         x_sc = keep.tile([P, S], U8, name="x_sc", align_bytes=64)
         nc.vector.tensor_copy(x_sc[:], scale_table[:].indirect(offsets[:]))
         w1_q = [quantize_first(w1_raw[g], f"w1_{g}", (VEC_M_FIRST, VEC_M)[g]) for g in range(PASSES)]

@@ -1,7 +1,6 @@
 from contextlib import ExitStack
 
 import concourse.mybir as mybir
-from concourse.masks import make_identity
 
 K, T, S, H, N = 1024, 1024, 512, 512, 256
 FLOPS = 2 * S * (2 * K * H + H * N)
@@ -22,11 +21,11 @@ K_PASS = P * PACK
 PASSES = K // K_PASS
 CHUNK = 128
 CHUNKS = S // CHUNK
+PAIR = 2 * CHUNK
 BLOCKS = N // P
 VEC_M = 80
 VEC_M_FIRST = 72
 VEC_M_BUSY = 84
-PIECES = ((0, CHUNK), (CHUNK, 2 * CHUNK), (2 * CHUNK, S))
 
 
 def tile_picked_modres_glusilu_p_kernel(
@@ -41,12 +40,9 @@ def tile_picked_modres_glusilu_p_kernel(
 
         scale_table = keep.tile([P, T], U8, name="scale_table", align_bytes=64)
         nc.vector.memset(scale_table[:].bitcast(I32), 0)
-        gate_rows = keep.tile([P, P], F32, name="gate_rows")
-        nc.gpsimd.memset(gate_rows[:], 0.0)
-        ident = keep.tile([P, P], F32, name="ident")
-        make_identity(nc, ident[:])
-        warm = keep.tile([P, 1], F32, name="warm")
-        nc.scalar.activation(warm[:], ident[:, 0:1], ACT.Silu)
+        warm = keep.tile([P, 2], F32, name="warm")
+        nc.gpsimd.memset(warm[:, 0:1], 0.0)
+        nc.scalar.activation(warm[:, 1:2], warm[:, 0:1], ACT.Silu)
 
         word_tables = [keep.tile([P, T], U32, name=f"word_table{g}", align_bytes=64) for g in range(PASSES)]
 
@@ -62,20 +58,20 @@ def tile_picked_modres_glusilu_p_kernel(
                 x_scales[:, 4 * q : 4 * q + 4, :].bitcast(I32),
             )
 
-
         def load_rows(w, g, name):
             raw = keep.tile([P, PACK, w.shape[1]], F32, name=name, tag=name, align_bytes=64)
             nc.sync.dma_start(raw[:], w[g * K_PASS : (g + 1) * K_PASS, :].rearrange("(p j) c -> p j c", j=PACK))
             return raw
 
         w1_raw = [load_rows(w1, g, f"w1_raw{g}") for g in range(PASSES)]
-        nc.sync.dma_start(gate_rows[0:CHUNKS, :], gate[0].rearrange("(c p) -> c p", p=P))
         w3_raw = [load_rows(w3, 0, "w3_raw0")]
         w3_halves = [load_rows(w3[:, u * H // 2 : (u + 1) * H // 2], 1, f"w3_half{u}") for u in range(2)]
+        w2_raw = load_rows(w2, 0, "w2_raw")
         res_tiles = [keep.tile([P, T], F32, name=f"res{b}") for b in range(BLOCKS)]
-        nc.sync.dma_start(res_tiles[0][:], res[0:P, :])
-        w2_raw = [load_rows(w2[:, b * P : (b + 1) * P], 0, f"w2_raw{b}") for b in range(BLOCKS)]
         nc.sync.dma_start(res_tiles[1][:], res[P : 2 * P, :])
+        gate_all = keep.tile([P, S], F32, name="gate_all")
+        nc.sync.dma_start(gate_all[:], gate)
+        nc.sync.dma_start(res_tiles[0][:], res[0:P, :])
 
         def quantize(grouped, width, name):
             codes = keep.tile([P, width], U32, name=name + "_codes", align_bytes=64)
@@ -107,12 +103,7 @@ def tile_picked_modres_glusilu_p_kernel(
         nc.scalar.copy(dst[:, P // 2 + VEC_M // 2 :], src[1][:, VEC_M // 2 :])
         w3_q.append(quantize(grouped[:], H, "w3_1"))
 
-        gate_bank = psum.tile([P, P], F32, name="gate_bank", tag="act3")
-        nc.tensor.transpose(gate_bank[:], gate_rows[:], ident[:])
-        gate_col = keep.tile([P, CHUNKS], F32, name="gate_col")
-        nc.scalar.copy(gate_col[:], gate_bank[:, 0:CHUNKS])
-
-        def first_product(w_q, c, tag, by_pass=False):
+        def first_product(w_q, c, tag, by_pass):
             bank = psum.tile([P, PACK, CHUNK], F32, name=tag, tag=tag)
             cols = slice(c * CHUNK, (c + 1) * CHUNK)
             steps = [(t, g) for t in range(PACK) for g in range(PASSES)]
@@ -132,76 +123,71 @@ def tile_picked_modres_glusilu_p_kernel(
                 )
             return bank[:].rearrange("p t n -> p n t")
 
-        early = keep.tile([P, S // 2 * PACK], F32, name="silu_early", tag="w3_raw0", align_bytes=64)
-        late = keep.tile([P, PACK * H], F32, name="late", tag="w3_half1", align_bytes=64)
-        later = late[:, : S // 2 * PACK]
+        early = keep.tile([P, 2 * S], F32, name="silu_early", tag="w3_raw0", align_bytes=64)
+        third = keep.tile([P, S], F32, name="silu_third", tag="w3_half1", align_bytes=64)
+
+        w2_bf16 = keep.tile([P, N * PACK], BF16, name="w2_bf16", align_bytes=64)
+        nc.scalar.copy(
+            w2_bf16[:].rearrange("p (c i j) -> p c j i", i=4, j=PACK),
+            w2_raw[:].rearrange("p j (c i) -> p c j i", i=4),
+        )
+        late = keep.tile([P, 2 * S], F32, name="late", tag="w2_raw", align_bytes=64)
+        homes = [early[:, :S], early[:, S:], third[:], late[:, :S]]
         gates = []
         for c in range(CHUNKS):
-            pre = first_product(w1_q, c, f"act{c % 2}", by_pass=True)
-            at = c % 2 * CHUNK * PACK
-            act = (early if c < 2 else later)[:, at : at + CHUNK * PACK].rearrange("p (n t) -> p n t", t=PACK)
+            pre = first_product(w1_q, c, f"act{c % 2}", True)
+            act = homes[c].rearrange("p (n t) -> p n t", t=PACK)
             nc.scalar.activation(act, pre, ACT.Silu)
             gates.append(act)
 
-        old = [late[:, 2 * S : 3 * S]]
-        nc.vector.tensor_copy(old[0], res_tiles[0][:].indirect(offsets[:]))
+        old0 = keep.tile([P, S], F32, name="old0")
+        old = [old0[:], late[:, S:]]
+        for b in (1, 0):
+            nc.scalar.activation(old[b], res_tiles[b][:].indirect(offsets[:]), ACT.Copy)
 
-        w2_bf16 = late[:, 3 * S :].bitcast(BF16)
-        for b in range(BLOCKS):
-            nc.scalar.copy(
-                w2_bf16[:, b * P * PACK : (b + 1) * P * PACK].rearrange("p (c i j) -> p c j i", i=4, j=PACK),
-                w2_raw[b][:].rearrange("p j (c i) -> p c j i", i=4),
+        w2_codes, w2_scales = quantize(w2_bf16[:], N, "w2")
+        ups = [first_product(w3_q, c, f"up{c}", True) for c in range(CHUNKS)]
+        gated = [[keep.tile([P, PAIR], F32, name=f"gated{u}{b}") for b in range(BLOCKS)] for u in range(2)]
+        h_codes = []
+        for u in range(2):
+            h = keep.tile([P, PAIR, PACK], BF16, name=f"h{u}", align_bytes=64)
+            for e in range(2):
+                nc.vector.tensor_tensor(h[:, e * CHUNK : (e + 1) * CHUNK, :], ups[2 * u + e], gates[2 * u + e], ALU.mult)
+            h_codes.append(quantize(h[:].rearrange("p n t -> p (n t)"), PAIR, f"h{u}"))
+
+        def scatter_on_vector(first, last):
+            u = first // PAIR
+            nc.vector.tensor_tensor(
+                res_tiles[0][:].indirect(offsets[:, first // 16 : last // 16]),
+                old[0][:, first:last],
+                gated[u][0][:, first - u * PAIR : last - u * PAIR],
+                ALU.add,
             )
 
-        w2_q = []
-        gated = [keep.tile([P, BLOCKS, last - first], F32, name=f"gated{first}") for first, last in PIECES]
-
-        def hidden(c):
-            up = first_product(w3_q, c, f"up{c}", by_pass=c >= 2)
-            h = keep.tile([P, CHUNK, PACK], BF16, name=f"h{c}", tag="w2_raw1" if c == 2 else f"h{c}", align_bytes=64)
-            nc.vector.tensor_tensor(h[:], up, gates[c], ALU.mult)
-            return h
-
-        def second_product(c, h):
-            h_codes, h_scales = quantize(h[:].rearrange("p n t -> p (n t)"), CHUNK, f"h{c}")
-            w2_codes, w2_scales = w2_q[0]
-            bank = psum.tile([P, 2, N], F32, name=f"down{c}", tag=f"act{c}")
-            nc.tensor.matmul_mx(
-                out=bank[:, 0, :],
-                lhsT=h_codes[:].bitcast(FP8X4),
-                lhsT_scale=h_scales[:],
-                rhs=w2_codes[:].bitcast(FP8X4),
-                rhs_scale=w2_scales[:],
-                start=True,
-                stop=True,
-            )
-            y_rows = keep.tile([P, N], F32, name=f"y_rows{c}")
-            nc.scalar.activation(y_rows[:], bank[:, 0, :], ACT.Copy, scale=gate_col[:, c : c + 1])
-            for b in range(BLOCKS):
-                nc.tensor.transpose(bank[:, 1, b * P : (b + 1) * P], y_rows[:, b * P : (b + 1) * P], ident[:])
-            piece = min(c, len(PIECES) - 1)
-            at = c * CHUNK - PIECES[piece][0]
-            nc.scalar.copy(
-                gated[piece][:, :, at : at + CHUNK],
-                bank[:, 1, :].rearrange("p (b n) -> p b n", b=BLOCKS),
-            )
-
-        h_bf16 = []
-        for c in range(CHUNKS):
-            h_bf16.append(hidden(c))
-            if c == 0:
-                w2_q.append(quantize(w2_bf16, N, "w2"))
-            else:
-                second_product(c - 1, h_bf16[c - 1])
-        old.append(late[:, 3 * S :])
-        nc.vector.tensor_copy(old[1], res_tiles[1][:].indirect(offsets[:]))
-        second_product(CHUNKS - 1, h_bf16[CHUNKS - 1])
-
-        for piece, (first, last) in enumerate(PIECES):
-            entries = offsets[:, first // 16 : last // 16]
-            for b in range(BLOCKS):
-                nc.vector.tensor_tensor(
-                    res_tiles[b][:].indirect(entries), old[b][:, first:last], gated[piece][:, b, :], ALU.add
+        for u in range(2):
+            codes, scales = h_codes[u]
+            cols = slice(u * PAIR, (u + 1) * PAIR)
+            bank = psum.tile([P, BLOCKS, PAIR], F32, name=f"down{u}")
+            for b in (1, 0):
+                nc.tensor.matmul_mx(
+                    out=bank[:, b, :],
+                    lhsT=w2_codes[:, b * P : (b + 1) * P].bitcast(FP8X4),
+                    lhsT_scale=w2_scales[:, b * P : (b + 1) * P],
+                    rhs=codes[:].bitcast(FP8X4),
+                    rhs_scale=scales[:],
+                    start=True,
+                    stop=True,
                 )
-        for b in range(BLOCKS):
+            for b in (1, 0):
+                nc.vector.tensor_tensor(gated[u][b][:], bank[:, b, :], gate_all[:, cols], ALU.mult)
+            summed = keep.tile([P, PAIR], F32, name=f"summed{u}")
+            nc.vector.tensor_tensor(summed[:], gated[u][1][:], old[1][:, cols], ALU.add)
+            nc.scalar.activation(
+                res_tiles[1][:].indirect(offsets[:, u * PAIR // 16 : (u + 1) * PAIR // 16]), summed[:], ACT.Copy
+            )
+            if u == 0:
+                scatter_on_vector(0, CHUNK)
+        scatter_on_vector(CHUNK, PAIR)
+        scatter_on_vector(PAIR, S)
+        for b in (1, 0):
             nc.sync.dma_start(out[b * P : (b + 1) * P, :], res_tiles[b][:])

@@ -23,6 +23,7 @@ CHUNK = 128
 CHUNKS = S // CHUNK
 PAIR = 2 * CHUNK
 BLOCKS = N // P
+FILL = 64
 VEC_M = 80
 VEC_M_FIRST = 72
 VEC_M_BUSY = 84
@@ -95,20 +96,27 @@ def tile_picked_modres_glusilu_p_kernel(
         w1_q = [quantize_first(w1_raw[g], f"w1_{g}", (VEC_M_FIRST, VEC_M)[g]) for g in range(PASSES)]
 
         w3_q = [quantize_first(w3_raw[0], "w3_0", VEC_M_BUSY)]
-        grouped = keep.tile([P, H * PACK], BF16, name="w3_1_bf16", align_bytes=64)
+        grouped = keep.tile([P, H * PACK], BF16, name="w3_1_bf16", tag="w3_1_bf16", align_bytes=64)
         dst = grouped[:].rearrange("p (t m j) -> p m j t", t=PACK, j=PACK)
         src = [half[:].rearrange("p j (m t) -> p m j t", t=PACK) for half in w3_halves]
         nc.vector.tensor_copy(dst[:, : P // 2], src[0])
         nc.vector.tensor_copy(dst[:, P // 2 : P // 2 + VEC_M // 2], src[1][:, : VEC_M // 2])
         nc.scalar.copy(dst[:, P // 2 + VEC_M // 2 :], src[1][:, VEC_M // 2 :])
-        w3_q.append(quantize(grouped[:], H, "w3_1"))
+        last_codes = keep.tile([P, H], U32, name="w3_1_codes", align_bytes=64)
+        last_scales = keep.tile([P, H], U8, name="w3_1_scales", align_bytes=64)
+        for u in range(2):
+            chans = slice(u * H // 2, (u + 1) * H // 2)
+            nc.vector.quantize_mx(
+                out=last_codes[:, chans].bitcast(FP8X4),
+                scales=last_scales[:, chans],
+                in_=grouped[:, u * H * PACK // 2 : (u + 1) * H * PACK // 2],
+            )
+        w3_q.append((last_codes, last_scales))
 
-        def first_product(w_q, c, tag, by_pass):
+        def first_product(w_q, c, tag, last_order):
             bank = psum.tile([P, PACK, CHUNK], F32, name=tag, tag=tag)
             cols = slice(c * CHUNK, (c + 1) * CHUNK)
-            steps = [(t, g) for t in range(PACK) for g in range(PASSES)]
-            if by_pass:
-                steps = [(t, g) for g in range(PASSES) for t in range(PACK)]
+            steps = [(t, 0) for t in range(PACK)] + [(t, 1) for t in last_order]
             for t, g in steps:
                 chans = slice(t * P, (t + 1) * P)
                 codes, scales = w_q[g]
@@ -118,76 +126,96 @@ def tile_picked_modres_glusilu_p_kernel(
                     lhsT_scale=scales[:, chans],
                     rhs=x_codes[g][:, cols].bitcast(FP8X4),
                     rhs_scale=x_sc[4 * g :, cols],
-                    start=(t, g) == steps[0] if by_pass else g == 0,
-                    stop=(t, g) == steps[-1] if by_pass else g == PASSES - 1,
+                    start=(t, g) == steps[0],
+                    stop=(t, g) == steps[-1],
                 )
             return bank[:].rearrange("p t n -> p n t")
 
         early = keep.tile([P, 2 * S], F32, name="silu_early", tag="w3_raw0", align_bytes=64)
-        third = keep.tile([P, S], F32, name="silu_third", tag="w3_half1", align_bytes=64)
+        late = keep.tile([P, 2 * S], F32, name="silu_late", tag="w3_half1", align_bytes=64)
 
-        w2_bf16 = keep.tile([P, N * PACK], BF16, name="w2_bf16", align_bytes=64)
-        nc.scalar.copy(
-            w2_bf16[:].rearrange("p (c i j) -> p c j i", i=4, j=PACK),
-            w2_raw[:].rearrange("p j (c i) -> p c j i", i=4),
-        )
-        late = keep.tile([P, 2 * S], F32, name="late", tag="w2_raw", align_bytes=64)
-        homes = [early[:, :S], early[:, S:], third[:], late[:, :S]]
-        gates = []
-        for c in range(CHUNKS):
-            pre = first_product(w1_q, c, f"act{c % 2}", True)
-            act = homes[c].rearrange("p (n t) -> p n t", t=PACK)
+        def gate_values(c, home):
+            pre = first_product(w1_q, c, f"act{c}", range(PACK))
+            act = home.rearrange("p (n t) -> p n t", t=PACK)
             nc.scalar.activation(act, pre, ACT.Silu)
-            gates.append(act)
+            return act
 
-        old0 = keep.tile([P, S], F32, name="old0")
-        old = [old0[:], late[:, S:]]
+        gates = [gate_values(c, home) for c, home in enumerate((early[:, :S], early[:, S:], late[:, :S]))]
+        w2_bf16 = keep.tile([P, N * PACK], BF16, name="w2_bf16", tag="w3_1_bf16", align_bytes=64)
+        nc.scalar.copy(
+            w2_bf16[:, : P * PACK].rearrange("p (c i j) -> p c j i", i=4, j=PACK),
+            w2_raw[:, :, :P].rearrange("p j (c i) -> p c j i", i=4),
+        )
+        nc.gpsimd.tensor_scalar(
+            w2_bf16[:, P * PACK :].rearrange("p (c j) -> p c j", j=PACK),
+            w2_raw[:, :, P:].rearrange("p j c -> p c j"),
+            1.0,
+            0.0,
+            ALU.mult,
+            ALU.add,
+        )
+        gates.append(gate_values(3, late[:, S:]))
+
+        old = [keep.tile([P, S], F32, name=f"old{b}")[:] for b in range(BLOCKS)]
         for b in (1, 0):
             nc.scalar.activation(old[b], res_tiles[b][:].indirect(offsets[:]), ACT.Copy)
 
-        w2_codes, w2_scales = quantize(w2_bf16[:], N, "w2")
-        ups = [first_product(w3_q, c, f"up{c}", True) for c in range(CHUNKS)]
-        gated = [[keep.tile([P, PAIR], F32, name=f"gated{u}{b}") for b in range(BLOCKS)] for u in range(2)]
-        h_codes = []
-        for u in range(2):
-            h = keep.tile([P, PAIR, PACK], BF16, name=f"h{u}", align_bytes=64)
-            for e in range(2):
-                nc.vector.tensor_tensor(h[:, e * CHUNK : (e + 1) * CHUNK, :], ups[2 * u + e], gates[2 * u + e], ALU.mult)
-            h_codes.append(quantize(h[:].rearrange("p n t -> p (n t)"), PAIR, f"h{u}"))
+        ups = [first_product(w3_q, c, f"up{c}", range(PACK) if c == 0 else range(PACK - 1, -1, -1)) for c in range(CHUNKS)]
+        h_homes = [keep.tile([P, PAIR * PACK], BF16, name=f"h{u}", align_bytes=64)[:] for u in range(2)]
+        gated = [keep.tile([P, S], F32, name=f"gated{b}") for b in range(BLOCKS)]
+        summed = keep.tile([P, S], F32, name="summed")
+        down = [[psum.tile([P, PAIR], F32, name=f"down{b}{u}", tag=f"act{2 * u + b}") for u in range(2)] for b in range(BLOCKS)]
 
-        def scatter_on_vector(first, last):
-            u = first // PAIR
-            nc.vector.tensor_tensor(
-                res_tiles[0][:].indirect(offsets[:, first // 16 : last // 16]),
-                old[0][:, first:last],
-                gated[u][0][:, first - u * PAIR : last - u * PAIR],
-                ALU.add,
-            )
+        def hidden(c):
+            h = h_homes[c // 2].rearrange("p (n t) -> p n t", t=PACK)
+            nc.vector.tensor_tensor(h[:, c % 2 * CHUNK : (c % 2 + 1) * CHUNK, :], ups[c], gates[c], ALU.mult)
 
-        for u in range(2):
-            codes, scales = h_codes[u]
-            cols = slice(u * PAIR, (u + 1) * PAIR)
-            bank = psum.tile([P, BLOCKS, PAIR], F32, name=f"down{u}")
+        def second_product(u, codes, scales):
             for b in (1, 0):
                 nc.tensor.matmul_mx(
-                    out=bank[:, b, :],
+                    out=down[b][u][:],
                     lhsT=w2_codes[:, b * P : (b + 1) * P].bitcast(FP8X4),
                     lhsT_scale=w2_scales[:, b * P : (b + 1) * P],
-                    rhs=codes[:].bitcast(FP8X4),
-                    rhs_scale=scales[:],
+                    rhs=codes.bitcast(FP8X4),
+                    rhs_scale=scales,
                     start=True,
                     stop=True,
                 )
-            for b in (1, 0):
-                nc.vector.tensor_tensor(gated[u][b][:], bank[:, b, :], gate_all[:, cols], ALU.mult)
-            summed = keep.tile([P, PAIR], F32, name=f"summed{u}")
-            nc.vector.tensor_tensor(summed[:], gated[u][1][:], old[1][:, cols], ALU.add)
-            nc.scalar.activation(
-                res_tiles[1][:].indirect(offsets[:, u * PAIR // 16 : (u + 1) * PAIR // 16]), summed[:], ACT.Copy
+
+        def apply_gate(b, cols):
+            nc.vector.tensor_tensor(gated[b][:, cols], down[b][cols.start // PAIR][:], gate_all[:, cols], ALU.mult)
+
+        def sum_and_scatter_on_scalar(cols):
+            nc.vector.tensor_tensor(summed[:, cols], gated[1][:, cols], old[1][:, cols], ALU.add)
+            entries = offsets[:, cols.start // 16 : cols.stop // 16]
+            nc.scalar.activation(res_tiles[1][:].indirect(entries), summed[:, cols], ACT.Copy)
+
+        def scatter_on_vector(first, last):
+            nc.vector.tensor_tensor(
+                res_tiles[0][:].indirect(offsets[:, first // 16 : last // 16]),
+                old[0][:, first:last],
+                gated[0][:, first:last],
+                ALU.add,
             )
-            if u == 0:
-                scatter_on_vector(0, CHUNK)
-        scatter_on_vector(CHUNK, PAIR)
-        scatter_on_vector(PAIR, S)
+
+        first_pair, second_pair = slice(0, PAIR), slice(PAIR, S)
+        hidden(0)
+        hidden(1)
+        w2_codes, w2_scales = quantize(w2_bf16[:], N, "w2")
+        h_codes, h_scales = quantize(h_homes[0], PAIR, "h0")
+        second_product(0, h_codes[:], h_scales[:])
+        hidden(2)
+        hidden(3)
+        apply_gate(1, first_pair)
+        last_h_codes, last_h_scales = quantize(h_homes[1], PAIR, "h1")
+        second_product(1, last_h_codes[:], last_h_scales[:])
+        sum_and_scatter_on_scalar(first_pair)
+        apply_gate(0, first_pair)
+        scatter_on_vector(0, FILL)
+        apply_gate(1, second_pair)
+        apply_gate(0, second_pair)
+        sum_and_scatter_on_scalar(second_pair)
+        scatter_on_vector(FILL, S - CHUNK)
+        scatter_on_vector(S - CHUNK, S)
         for b in (1, 0):
             nc.sync.dma_start(out[b * P : (b + 1) * P, :], res_tiles[b][:])

@@ -24,6 +24,7 @@ CHUNKS = S // CHUNK
 PAIR = 2 * CHUNK
 BLOCKS = N // P
 FILL = 64
+W2_ON_SCALAR = 64
 VEC_M = 80
 VEC_M_FIRST = 72
 VEC_M_BUSY = 84
@@ -70,9 +71,9 @@ def tile_picked_modres_glusilu_p_kernel(
         w2_raw = load_rows(w2, 0, "w2_raw")
         res_tiles = [keep.tile([P, T], F32, name=f"res{b}") for b in range(BLOCKS)]
         nc.sync.dma_start(res_tiles[1][:], res[P : 2 * P, :])
+        nc.sync.dma_start(res_tiles[0][:], res[0:P, :])
         gate_all = keep.tile([P, S], F32, name="gate_all")
         nc.sync.dma_start(gate_all[:], gate)
-        nc.sync.dma_start(res_tiles[0][:], res[0:P, :])
 
         def quantize(grouped, width, name):
             codes = keep.tile([P, width], U32, name=name + "_codes", align_bytes=64)
@@ -143,12 +144,12 @@ def tile_picked_modres_glusilu_p_kernel(
         gates = [gate_values(c, home) for c, home in enumerate((early[:, :S], early[:, S:], late[:, :S]))]
         w2_bf16 = keep.tile([P, N * PACK], BF16, name="w2_bf16", tag="w3_1_bf16", align_bytes=64)
         nc.scalar.copy(
-            w2_bf16[:, : P * PACK].rearrange("p (c i j) -> p c j i", i=4, j=PACK),
-            w2_raw[:, :, :P].rearrange("p j (c i) -> p c j i", i=4),
+            w2_bf16[:, : W2_ON_SCALAR * PACK].rearrange("p (c i j) -> p c j i", i=4, j=PACK),
+            w2_raw[:, :, :W2_ON_SCALAR].rearrange("p j (c i) -> p c j i", i=4),
         )
         nc.gpsimd.tensor_scalar(
-            w2_bf16[:, P * PACK :].rearrange("p (c j) -> p c j", j=PACK),
-            w2_raw[:, :, P:].rearrange("p j c -> p c j"),
+            w2_bf16[:, W2_ON_SCALAR * PACK :].rearrange("p (c j) -> p c j", j=PACK),
+            w2_raw[:, :, W2_ON_SCALAR:].rearrange("p j c -> p c j"),
             1.0,
             0.0,
             ALU.mult,

@@ -36,6 +36,7 @@ def tile_picked_modres_glusilu_p_kernel(
     nc = tc.nc
     with ExitStack() as ctx:
         keep = ctx.enter_context(tc.tile_pool(name="keep", bufs=1))
+        shared = ctx.enter_context(tc.tile_pool(name="shared", bufs=1))
         psum = ctx.enter_context(tc.psum_pool(name="psum", bufs=1))
 
         offsets = keep.tile([P, S // 16], U16, name="offsets")
@@ -68,12 +69,13 @@ def tile_picked_modres_glusilu_p_kernel(
         w1_raw = [load_rows(w1, g, f"w1_raw{g}") for g in range(PASSES)]
         w3_raw = [load_rows(w3, 0, "w3_raw0")]
         w3_halves = [load_rows(w3[:, u * H // 2 : (u + 1) * H // 2], 1, f"w3_half{u}") for u in range(2)]
-        w2_raw = load_rows(w2, 0, "w2_raw")
+        w2_raw = shared.tile([P, PACK, N], F32, name="w2_raw", offset=0, align_bytes=64)
+        nc.sync.dma_start(w2_raw[:], w2.rearrange("(p j) c -> p j c", j=PACK))
         res_tiles = [keep.tile([P, T], F32, name=f"res{b}") for b in range(BLOCKS)]
         nc.sync.dma_start(res_tiles[1][:], res[P : 2 * P, :])
-        nc.sync.dma_start(res_tiles[0][:], res[0:P, :])
         gate_all = keep.tile([P, S], F32, name="gate_all")
         nc.sync.dma_start(gate_all[:], gate)
+        nc.sync.dma_start(res_tiles[0][:], res[0:P, :])
 
         def quantize(grouped, width, name):
             codes = keep.tile([P, width], U32, name=name + "_codes", align_bytes=64)
@@ -97,22 +99,6 @@ def tile_picked_modres_glusilu_p_kernel(
         w1_q = [quantize_first(w1_raw[g], f"w1_{g}", (VEC_M_FIRST, VEC_M)[g]) for g in range(PASSES)]
 
         w3_q = [quantize_first(w3_raw[0], "w3_0", VEC_M_BUSY)]
-        grouped = keep.tile([P, H * PACK], BF16, name="w3_1_bf16", tag="w3_1_bf16", align_bytes=64)
-        dst = grouped[:].rearrange("p (t m j) -> p m j t", t=PACK, j=PACK)
-        src = [half[:].rearrange("p j (m t) -> p m j t", t=PACK) for half in w3_halves]
-        nc.vector.tensor_copy(dst[:, : P // 2], src[0])
-        nc.vector.tensor_copy(dst[:, P // 2 : P // 2 + VEC_M // 2], src[1][:, : VEC_M // 2])
-        nc.scalar.copy(dst[:, P // 2 + VEC_M // 2 :], src[1][:, VEC_M // 2 :])
-        last_codes = keep.tile([P, H], U32, name="w3_1_codes", align_bytes=64)
-        last_scales = keep.tile([P, H], U8, name="w3_1_scales", align_bytes=64)
-        for u in range(2):
-            chans = slice(u * H // 2, (u + 1) * H // 2)
-            nc.vector.quantize_mx(
-                out=last_codes[:, chans].bitcast(FP8X4),
-                scales=last_scales[:, chans],
-                in_=grouped[:, u * H * PACK // 2 : (u + 1) * H * PACK // 2],
-            )
-        w3_q.append((last_codes, last_scales))
 
         def first_product(w_q, c, tag, last_order):
             bank = psum.tile([P, PACK, CHUNK], F32, name=tag, tag=tag)
@@ -133,7 +119,6 @@ def tile_picked_modres_glusilu_p_kernel(
             return bank[:].rearrange("p t n -> p n t")
 
         early = keep.tile([P, 2 * S], F32, name="silu_early", tag="w3_raw0", align_bytes=64)
-        late = keep.tile([P, 2 * S], F32, name="silu_late", tag="w3_half1", align_bytes=64)
 
         def gate_values(c, home):
             pre = first_product(w1_q, c, f"act{c}", range(PACK))
@@ -141,7 +126,32 @@ def tile_picked_modres_glusilu_p_kernel(
             nc.scalar.activation(act, pre, ACT.Silu)
             return act
 
-        gates = [gate_values(c, home) for c, home in enumerate((early[:, :S], early[:, S:], late[:, :S]))]
+        gates = [gate_values(c, home) for c, home in enumerate((early[:, :S], early[:, S:]))]
+        grouped = keep.tile([P, H * PACK], BF16, name="w3_1_bf16", tag="w3_1_bf16", align_bytes=64)
+        dst = grouped[:].rearrange("p (t m j) -> p m j t", t=PACK, j=PACK)
+        src = [half[:].rearrange("p j (m t) -> p m j t", t=PACK) for half in w3_halves]
+        last_codes = keep.tile([P, H], U32, name="w3_1_codes", align_bytes=64)
+        last_scales = keep.tile([P, H], U8, name="w3_1_scales", align_bytes=64)
+
+        def quantize_half(u):
+            for t in range(PACK):
+                chans = slice(t * P + u * P // 2, t * P + (u + 1) * P // 2)
+                nc.vector.quantize_mx(
+                    out=last_codes[:, chans].bitcast(FP8X4),
+                    scales=last_scales[:, chans],
+                    in_=grouped[:, chans.start * PACK : chans.stop * PACK],
+                )
+
+        for u in range(2):
+            first = u * P // 2
+            nc.vector.tensor_copy(dst[:, first : first + VEC_M // 2], src[u][:, : VEC_M // 2])
+            nc.scalar.copy(dst[:, first + VEC_M // 2 : first + P // 2], src[u][:, VEC_M // 2 :])
+        quantize_half(0)
+        quantize_half(1)
+        w3_q.append((last_codes, last_scales))
+
+        late = keep.tile([P, 2 * S], F32, name="silu_late", tag="w3_half1", align_bytes=64)
+        gates.append(gate_values(2, late[:, :S]))
         w2_bf16 = keep.tile([P, N * PACK], BF16, name="w2_bf16", tag="w3_1_bf16", align_bytes=64)
         nc.scalar.copy(
             w2_bf16[:, : W2_ON_SCALAR * PACK].rearrange("p (c i j) -> p c j i", i=4, j=PACK),
@@ -162,7 +172,7 @@ def tile_picked_modres_glusilu_p_kernel(
             nc.scalar.activation(old[b], res_tiles[b][:].indirect(offsets[:]), ACT.Copy)
 
         ups = [first_product(w3_q, c, f"up{c}", range(PACK) if c == 0 else range(PACK - 1, -1, -1)) for c in range(CHUNKS)]
-        h_homes = [keep.tile([P, PAIR * PACK], BF16, name=f"h{u}", align_bytes=64)[:] for u in range(2)]
+        h_homes = [keep.tile([P, PAIR * PACK], BF16, name="h0", align_bytes=64)[:]]
         gated = [keep.tile([P, S], F32, name=f"gated{b}") for b in range(BLOCKS)]
         summed = keep.tile([P, S], F32, name="summed")
         down = [[psum.tile([P, PAIR], F32, name=f"down{b}{u}", tag=f"act{2 * u + b}") for u in range(2)] for b in range(BLOCKS)]
@@ -203,8 +213,11 @@ def tile_picked_modres_glusilu_p_kernel(
         hidden(0)
         hidden(1)
         w2_codes, w2_scales = quantize(w2_bf16[:], N, "w2")
-        h_codes, h_scales = quantize(h_homes[0], PAIR, "h0")
+        h_codes = shared.tile([P, PAIR], U32, name="h0_codes", offset=2 * PAIR * PACK, align_bytes=64)
+        h_scales = keep.tile([P, PAIR], U8, name="h0_scales", align_bytes=64)
+        nc.vector.quantize_mx(out=h_codes[:].bitcast(FP8X4), scales=h_scales[:], in_=h_homes[0])
         second_product(0, h_codes[:], h_scales[:])
+        h_homes.append(shared.tile([P, PAIR * PACK], BF16, name="h1", offset=0, align_bytes=64)[:])
         hidden(2)
         hidden(3)
         apply_gate(1, first_pair)
@@ -216,7 +229,6 @@ def tile_picked_modres_glusilu_p_kernel(
         apply_gate(1, second_pair)
         apply_gate(0, second_pair)
         sum_and_scatter_on_scalar(second_pair)
-        scatter_on_vector(FILL, S - CHUNK)
-        scatter_on_vector(S - CHUNK, S)
-        for b in (1, 0):
-            nc.sync.dma_start(out[b * P : (b + 1) * P, :], res_tiles[b][:])
+        scatter_on_vector(FILL, S)
+        nc.sync.dma_start(out[P:, :], res_tiles[1][:])
+        nc.scalar.dma_start(out[:P, :], res_tiles[0][:])

@@ -27,7 +27,8 @@ FILL = 64
 W2_ON_SCALAR = 64
 VEC_M = 80
 VEC_M_FIRST = 72
-VEC_M_BUSY = 84
+VEC_M_BUSY = 80
+VEC_M_HALF = (60, 38)
 
 
 def tile_picked_modres_glusilu_p_kernel(
@@ -68,7 +69,11 @@ def tile_picked_modres_glusilu_p_kernel(
 
         w1_raw = [load_rows(w1, g, f"w1_raw{g}") for g in range(PASSES)]
         w3_raw = [load_rows(w3, 0, "w3_raw0")]
-        w3_halves = [load_rows(w3[:, u * H // 2 : (u + 1) * H // 2], 1, f"w3_half{u}") for u in range(2)]
+        w3_last = keep.tile([P, PACK * H], F32, name="w3_last", tag="w3_last", align_bytes=64)
+        w3_halves = w3_last[:].rearrange("p (u j c) -> p u j c", u=2, j=PACK)
+        for u in range(2):
+            rows = w3[K_PASS:, u * H // 2 : (u + 1) * H // 2]
+            nc.sync.dma_start(w3_halves[:, u], rows.rearrange("(p j) c -> p j c", j=PACK))
         w2_raw = shared.tile([P, PACK, N], F32, name="w2_raw", offset=0, align_bytes=64)
         nc.sync.dma_start(w2_raw[:], w2.rearrange("(p j) c -> p j c", j=PACK))
         res_tiles = [keep.tile([P, T], F32, name=f"res{b}") for b in range(BLOCKS)]
@@ -83,22 +88,34 @@ def tile_picked_modres_glusilu_p_kernel(
             nc.vector.quantize_mx(out=codes[:].bitcast(FP8X4), scales=scales[:], in_=grouped)
             return codes, scales
 
-        def quantize_first(raw, name, on_vector):
+        def quantize_first(raw, name, on_vector, steps):
             grouped = keep.tile([P, H * PACK], BF16, name=name + "_bf16", tag=name + "_bf16", align_bytes=64)
             dst = grouped[:].rearrange("p (t m j) -> p m j t", t=PACK, j=PACK)
             src = raw[:].rearrange("p j (m t) -> p m j t", t=PACK)
-            nc.vector.tensor_copy(dst[:, :on_vector], src[:, :on_vector])
-            nc.scalar.copy(dst[:, on_vector:], src[:, on_vector:])
-            return quantize(grouped[:], H, name)
+            codes = keep.tile([P, H], U32, name=name + "_codes", align_bytes=64)
+            scales = keep.tile([P, H], U8, name=name + "_scales", align_bytes=64)
+            width = PACK // steps
+            for i in range(steps):
+                tiles = slice(i * width, (i + 1) * width)
+                nc.vector.tensor_copy(dst[:, :on_vector, :, tiles], src[:, :on_vector, :, tiles])
+                nc.scalar.copy(dst[:, on_vector:, :, tiles], src[:, on_vector:, :, tiles])
+            for i in range(steps):
+                chans = slice(i * width * P, (i + 1) * width * P)
+                nc.vector.quantize_mx(
+                    out=codes[:, chans].bitcast(FP8X4),
+                    scales=scales[:, chans],
+                    in_=grouped[:, chans.start * PACK : chans.stop * PACK],
+                )
+            return codes, scales
 
         x_codes = [keep.tile([P, S], U32, name=f"x_codes{g}", align_bytes=64) for g in range(PASSES)]
         for g in range(PASSES):
             nc.vector.tensor_copy(x_codes[g][:], word_tables[g][:].indirect(offsets[:]))
         x_sc = keep.tile([P, S], U8, name="x_sc", align_bytes=64)
         nc.vector.tensor_copy(x_sc[:], scale_table[:].indirect(offsets[:]))
-        w1_q = [quantize_first(w1_raw[g], f"w1_{g}", (VEC_M_FIRST, VEC_M)[g]) for g in range(PASSES)]
+        w1_q = [quantize_first(w1_raw[g], f"w1_{g}", (VEC_M_FIRST, VEC_M)[g], 1 + g) for g in range(PASSES)]
 
-        w3_q = [quantize_first(w3_raw[0], "w3_0", VEC_M_BUSY)]
+        w3_q = [quantize_first(w3_raw[0], "w3_0", VEC_M_BUSY, 2)]
 
         def first_product(w_q, c, tag, last_order):
             bank = psum.tile([P, PACK, CHUNK], F32, name=tag, tag=tag)
@@ -129,7 +146,8 @@ def tile_picked_modres_glusilu_p_kernel(
         gates = [gate_values(c, home) for c, home in enumerate((early[:, :S], early[:, S:]))]
         grouped = keep.tile([P, H * PACK], BF16, name="w3_1_bf16", tag="w3_1_bf16", align_bytes=64)
         dst = grouped[:].rearrange("p (t m j) -> p m j t", t=PACK, j=PACK)
-        src = [half[:].rearrange("p j (m t) -> p m j t", t=PACK) for half in w3_halves]
+        dst = dst.rearrange("p (u m) j t -> p u m j t", u=2)
+        src = w3_halves.rearrange("p u j (m t) -> p u m j t", t=PACK)
         last_codes = keep.tile([P, H], U32, name="w3_1_codes", align_bytes=64)
         last_scales = keep.tile([P, H], U8, name="w3_1_scales", align_bytes=64)
 
@@ -142,15 +160,16 @@ def tile_picked_modres_glusilu_p_kernel(
                     in_=grouped[:, chans.start * PACK : chans.stop * PACK],
                 )
 
-        for u in range(2):
-            first = u * P // 2
-            nc.vector.tensor_copy(dst[:, first : first + VEC_M // 2], src[u][:, : VEC_M // 2])
-            nc.scalar.copy(dst[:, first + VEC_M // 2 : first + P // 2], src[u][:, VEC_M // 2 :])
+        wide, narrow = VEC_M_HALF
+        nc.vector.tensor_copy(dst[:, 0, :wide], src[:, 0, :wide])
+        nc.vector.tensor_copy(dst[:, 1, :narrow], src[:, 1, :narrow])
+        nc.scalar.copy(dst[:, :, wide:], src[:, :, wide:])
+        nc.scalar.copy(dst[:, 1, narrow:wide], src[:, 1, narrow:wide])
         quantize_half(0)
         quantize_half(1)
         w3_q.append((last_codes, last_scales))
 
-        late = keep.tile([P, 2 * S], F32, name="silu_late", tag="w3_half1", align_bytes=64)
+        late = keep.tile([P, 2 * S], F32, name="silu_late", tag="w3_last", align_bytes=64)
         gates.append(gate_values(2, late[:, :S]))
         w2_bf16 = keep.tile([P, N * PACK], BF16, name="w2_bf16", tag="w3_1_bf16", align_bytes=64)
         nc.scalar.copy(

@@ -23,7 +23,6 @@ CHUNK = 128
 CHUNKS = S // CHUNK
 PAIR = 2 * CHUNK
 BLOCKS = N // P
-FILL = 64
 W2_ON_SCALAR = 64
 VEC_M = 80
 VEC_M_FIRST = 72
@@ -186,13 +185,14 @@ def tile_picked_modres_glusilu_p_kernel(
         )
         gates.append(gate_values(3, late[:, S:]))
 
-        old = [keep.tile([P, S], F32, name=f"old{b}")[:] for b in range(BLOCKS)]
-        for b in (1, 0):
-            nc.scalar.activation(old[b], res_tiles[b][:].indirect(offsets[:]), ACT.Copy)
+        tail_home = keep.tile([P, 2 * S - CHUNK], F32, name="tail_home")
+        old = [tail_home[:, :S], keep.tile([P, S], F32, name="old1")[:]]
+        nc.scalar.activation(old[1], res_tiles[1][:].indirect(offsets[:]), ACT.Copy)
+        nc.scalar.activation(old[0][:, : S - CHUNK], res_tiles[0][:].indirect(offsets[:, : (S - CHUNK) // 16]), ACT.Copy)
 
         ups = [first_product(w3_q, c, f"up{c}", range(PACK) if c == 0 else range(PACK - 1, -1, -1)) for c in range(CHUNKS)]
         h_homes = [keep.tile([P, PAIR * PACK], BF16, name="h0", align_bytes=64)[:]]
-        gated = [keep.tile([P, S], F32, name=f"gated{b}") for b in range(BLOCKS)]
+        gated = [keep.tile([P, S], F32, name="gated0")[:], tail_home[:, S - CHUNK :]]
         summed = keep.tile([P, S], F32, name="summed")
         down = [[psum.tile([P, PAIR], F32, name=f"down{b}{u}", tag=f"act{2 * u + b}") for u in range(2)] for b in range(BLOCKS)]
 
@@ -244,10 +244,10 @@ def tile_picked_modres_glusilu_p_kernel(
         second_product(1, last_h_codes[:], last_h_scales[:])
         sum_and_scatter_on_scalar(first_pair)
         apply_gate(0, first_pair)
-        scatter_on_vector(0, FILL)
+        nc.vector.tensor_copy(old[0][:, S - CHUNK :], res_tiles[0][:].indirect(offsets[:, (S - CHUNK) // 16 :]))
         apply_gate(1, second_pair)
         apply_gate(0, second_pair)
         sum_and_scatter_on_scalar(second_pair)
-        scatter_on_vector(FILL, S)
+        scatter_on_vector(0, S)
         nc.sync.dma_start(out[P:, :], res_tiles[1][:])
         nc.scalar.dma_start(out[:P, :], res_tiles[0][:])

@@ -27,7 +27,7 @@ W2_ON_SCALAR = 64
 VEC_M = 80
 VEC_M_FIRST = 72
 VEC_M_BUSY = 80
-VEC_M_HALF = (60, 38)
+VEC_M_LAST = 38
 
 
 def tile_picked_modres_glusilu_p_kernel(
@@ -159,12 +159,13 @@ def tile_picked_modres_glusilu_p_kernel(
                     in_=grouped[:, chans.start * PACK : chans.stop * PACK],
                 )
 
-        wide, narrow = VEC_M_HALF
-        nc.vector.tensor_copy(dst[:, 0, :wide], src[:, 0, :wide])
-        nc.vector.tensor_copy(dst[:, 1, :narrow], src[:, 1, :narrow])
-        nc.scalar.copy(dst[:, :, wide:], src[:, :, wide:])
-        nc.scalar.copy(dst[:, 1, narrow:wide], src[:, 1, narrow:wide])
+        tile_pairs = (slice(0, 2), slice(2, PACK))
+        for tiles in tile_pairs:
+            nc.vector.tensor_copy(dst[:, 0, :, :, tiles], src[:, 0, :, :, tiles])
         quantize_half(0)
+        for tiles in tile_pairs:
+            nc.vector.tensor_copy(dst[:, 1, :VEC_M_LAST, :, tiles], src[:, 1, :VEC_M_LAST, :, tiles])
+            nc.scalar.copy(dst[:, 1, VEC_M_LAST:, :, tiles], src[:, 1, VEC_M_LAST:, :, tiles])
         quantize_half(1)
         w3_q.append((last_codes, last_scales))
 
@@ -250,4 +251,4 @@ def tile_picked_modres_glusilu_p_kernel(
         sum_and_scatter_on_scalar(second_pair)
         scatter_on_vector(0, S)
         nc.sync.dma_start(out[P:, :], res_tiles[1][:])
-        nc.scalar.dma_start(out[:P, :], res_tiles[0][:])
+        nc.sync.dma_start(out[:P, :], res_tiles[0][:])

@@ -78,8 +78,9 @@ def tile_picked_modres_glusilu_p_kernel(
         res_tiles = [keep.tile([P, T], F32, name=f"res{b}") for b in range(BLOCKS)]
         nc.sync.dma_start(res_tiles[1][:], res[P : 2 * P, :])
         gate_all = keep.tile([P, S], F32, name="gate_all")
-        nc.sync.dma_start(gate_all[:], gate)
+        nc.sync.dma_start(gate_all[:, :PAIR], gate[:, :PAIR])
         nc.sync.dma_start(res_tiles[0][:], res[0:P, :])
+        nc.sync.dma_start(gate_all[:, PAIR:], gate[:, PAIR:])
 
         def quantize(grouped, width, name):
             codes = keep.tile([P, width], U32, name=name + "_codes", align_bytes=64)

@@ -25,7 +25,7 @@ PAIR = 2 * CHUNK
 BLOCKS = N // P
 W2_ON_SCALAR = 64
 VEC_M = 80
-VEC_M_FIRST = 72
+VEC_M_FIRST = 48
 VEC_M_BUSY = 80
 VEC_M_LAST = 38
 
@@ -41,7 +41,7 @@ def tile_picked_modres_glusilu_p_kernel(
 
         offsets = keep.tile([P, S // 16], U16, name="offsets")
 
-        scale_table = keep.tile([P, T], U8, name="scale_table", align_bytes=64)
+        scale_table = keep.tile([P, T], U8, name="scale_table", tag="w1_0_codes", align_bytes=64)
         nc.vector.memset(scale_table[:].bitcast(I32), 0)
         warm = keep.tile([P, 2], F32, name="warm")
         nc.gpsimd.memset(warm[:, 0:1], 0.0)
@@ -55,18 +55,22 @@ def tile_picked_modres_glusilu_p_kernel(
         load_words(0)
         nc.sync.dma_start(offsets[:], offs)
         load_words(1)
-        for q in range(4):
-            nc.sync.dma_start(
-                scale_table[32 * q : 32 * q + 4 * PASSES, :].bitcast(I32),
-                x_scales[:, 4 * q : 4 * q + 4, :].bitcast(I32),
-            )
+
+        def load_scales(rows):
+            for r in rows:
+                for g in range(PASSES):
+                    nc.sync.dma_start(scale_table[4 * g + r : P : 32, :].bitcast(I32), x_scales[g, r:16:4, :].bitcast(I32))
+
+        load_scales((0, 1))
 
         def load_rows(w, g, name):
             raw = keep.tile([P, PACK, w.shape[1]], F32, name=name, tag=name, align_bytes=64)
             nc.sync.dma_start(raw[:], w[g * K_PASS : (g + 1) * K_PASS, :].rearrange("(p j) c -> p j c", j=PACK))
             return raw
 
-        w1_raw = [load_rows(w1, g, f"w1_raw{g}") for g in range(PASSES)]
+        w1_raw = [load_rows(w1, 0, "w1_raw0")]
+        load_scales((2, 3))
+        w1_raw.append(load_rows(w1, 1, "w1_raw1"))
         w3_raw = [load_rows(w3, 0, "w3_raw0")]
         w3_last = keep.tile([P, PACK * H], F32, name="w3_last", tag="w3_last", align_bytes=64)
         w3_halves = w3_last[:].rearrange("p (u j c) -> p u j c", u=2, j=PACK)
@@ -88,17 +92,21 @@ def tile_picked_modres_glusilu_p_kernel(
             nc.vector.quantize_mx(out=codes[:].bitcast(FP8X4), scales=scales[:], in_=grouped)
             return codes, scales
 
-        def quantize_first(raw, name, on_vector, steps):
+        def round_first(raw, name, on_vector, steps):
             grouped = keep.tile([P, H * PACK], BF16, name=name + "_bf16", tag=name + "_bf16", align_bytes=64)
             dst = grouped[:].rearrange("p (t m j) -> p m j t", t=PACK, j=PACK)
             src = raw[:].rearrange("p j (m t) -> p m j t", t=PACK)
-            codes = keep.tile([P, H], U32, name=name + "_codes", align_bytes=64)
-            scales = keep.tile([P, H], U8, name=name + "_scales", align_bytes=64)
             width = PACK // steps
             for i in range(steps):
                 tiles = slice(i * width, (i + 1) * width)
                 nc.vector.tensor_copy(dst[:, :on_vector, :, tiles], src[:, :on_vector, :, tiles])
                 nc.scalar.copy(dst[:, on_vector:, :, tiles], src[:, on_vector:, :, tiles])
+            return grouped
+
+        def quantize_first(grouped, name, steps):
+            codes = keep.tile([P, H], U32, name=name + "_codes", tag=name + "_codes", align_bytes=64)
+            scales = keep.tile([P, H], U8, name=name + "_scales", align_bytes=64)
+            width = PACK // steps
             for i in range(steps):
                 chans = slice(i * width * P, (i + 1) * width * P)
                 nc.vector.quantize_mx(
@@ -111,11 +119,13 @@ def tile_picked_modres_glusilu_p_kernel(
         x_codes = [keep.tile([P, S], U32, name=f"x_codes{g}", align_bytes=64) for g in range(PASSES)]
         for g in range(PASSES):
             nc.vector.tensor_copy(x_codes[g][:], word_tables[g][:].indirect(offsets[:]))
+        first = round_first(w1_raw[0], "w1_0", VEC_M_FIRST, 1)
         x_sc = keep.tile([P, S], U8, name="x_sc", align_bytes=64)
         nc.vector.tensor_copy(x_sc[:], scale_table[:].indirect(offsets[:]))
-        w1_q = [quantize_first(w1_raw[g], f"w1_{g}", (VEC_M_FIRST, VEC_M)[g], 1 + g) for g in range(PASSES)]
+        w1_q = [quantize_first(first, "w1_0", 2)]
+        w1_q.append(quantize_first(round_first(w1_raw[1], "w1_1", VEC_M, 2), "w1_1", 2))
 
-        w3_q = [quantize_first(w3_raw[0], "w3_0", VEC_M_BUSY, 2)]
+        w3_q = [quantize_first(round_first(w3_raw[0], "w3_0", VEC_M_BUSY, 2), "w3_0", 2)]
 
         def first_product(w_q, c, tag, last_order):
             bank = psum.tile([P, PACK, CHUNK], F32, name=tag, tag=tag)

@@ -25,7 +25,7 @@ PAIR = 2 * CHUNK
 BLOCKS = N // P
 W2_ON_SCALAR = 64
 VEC_M = 80
-VEC_M_FIRST = 48
+VEC_M_FIRST = 72
 VEC_M_BUSY = 80
 VEC_M_LAST = 38
 
@@ -41,7 +41,7 @@ def tile_picked_modres_glusilu_p_kernel(
 
         offsets = keep.tile([P, S // 16], U16, name="offsets")
 
-        scale_table = keep.tile([P, T], U8, name="scale_table", tag="w1_0_codes", align_bytes=64)
+        scale_table = keep.tile([P, T], U8, name="scale_table", align_bytes=64)
         nc.vector.memset(scale_table[:].bitcast(I32), 0)
         warm = keep.tile([P, 2], F32, name="warm")
         nc.gpsimd.memset(warm[:, 0:1], 0.0)
@@ -54,7 +54,6 @@ def tile_picked_modres_glusilu_p_kernel(
 
         load_words(0)
         nc.sync.dma_start(offsets[:], offs)
-        load_words(1)
 
         def load_scales(rows):
             for r in rows:
@@ -62,14 +61,18 @@ def tile_picked_modres_glusilu_p_kernel(
                     nc.sync.dma_start(scale_table[4 * g + r : P : 32, :].bitcast(I32), x_scales[g, r:16:4, :].bitcast(I32))
 
         load_scales((0, 1))
+        load_words(1)
 
         def load_rows(w, g, name):
             raw = keep.tile([P, PACK, w.shape[1]], F32, name=name, tag=name, align_bytes=64)
             nc.sync.dma_start(raw[:], w[g * K_PASS : (g + 1) * K_PASS, :].rearrange("(p j) c -> p j c", j=PACK))
             return raw
 
-        w1_raw = [load_rows(w1, 0, "w1_raw0")]
+        w1_raw = [keep.tile([P, PACK, H], F32, name="w1_raw0", align_bytes=64)]
+        w1_first = w1[:K_PASS, :].rearrange("(p j) c -> p j c", j=PACK)
+        nc.sync.dma_start(w1_raw[0][:, :2], w1_first[:, :2])
         load_scales((2, 3))
+        nc.sync.dma_start(w1_raw[0][:, 2:], w1_first[:, 2:])
         w1_raw.append(load_rows(w1, 1, "w1_raw1"))
         w3_raw = [load_rows(w3, 0, "w3_raw0")]
         w3_last = keep.tile([P, PACK * H], F32, name="w3_last", tag="w3_last", align_bytes=64)
@@ -119,10 +122,9 @@ def tile_picked_modres_glusilu_p_kernel(
         x_codes = [keep.tile([P, S], U32, name=f"x_codes{g}", align_bytes=64) for g in range(PASSES)]
         for g in range(PASSES):
             nc.vector.tensor_copy(x_codes[g][:], word_tables[g][:].indirect(offsets[:]))
-        first = round_first(w1_raw[0], "w1_0", VEC_M_FIRST, 1)
         x_sc = keep.tile([P, S], U8, name="x_sc", align_bytes=64)
         nc.vector.tensor_copy(x_sc[:], scale_table[:].indirect(offsets[:]))
-        w1_q = [quantize_first(first, "w1_0", 2)]
+        w1_q = [quantize_first(round_first(w1_raw[0], "w1_0", VEC_M_FIRST, 1), "w1_0", 1)]
         w1_q.append(quantize_first(round_first(w1_raw[1], "w1_1", VEC_M, 2), "w1_1", 2))
 
         w3_q = [quantize_first(round_first(w3_raw[0], "w3_0", VEC_M_BUSY, 2), "w3_0", 2)]
@@ -197,14 +199,13 @@ def tile_picked_modres_glusilu_p_kernel(
         )
         gates.append(gate_values(3, late[:, S:]))
 
-        tail_home = keep.tile([P, 2 * S - CHUNK], F32, name="tail_home")
-        old = [tail_home[:, :S], keep.tile([P, S], F32, name="old1")[:]]
+        old = [keep.tile([P, S], F32, name=f"old{b}")[:] for b in range(BLOCKS)]
         nc.scalar.activation(old[1], res_tiles[1][:].indirect(offsets[:]), ACT.Copy)
-        nc.scalar.activation(old[0][:, : S - CHUNK], res_tiles[0][:].indirect(offsets[:, : (S - CHUNK) // 16]), ACT.Copy)
+        nc.scalar.activation(old[0], res_tiles[0][:].indirect(offsets[:]), ACT.Copy)
 
         ups = [first_product(w3_q, c, f"up{c}", range(PACK) if c == 0 else range(PACK - 1, -1, -1)) for c in range(CHUNKS)]
         h_homes = [keep.tile([P, PAIR * PACK], BF16, name="h0", align_bytes=64)[:]]
-        gated = [keep.tile([P, S], F32, name="gated0")[:], tail_home[:, S - CHUNK :]]
+        gated = [keep.tile([P, S], F32, name=f"gated{b}")[:] for b in range(BLOCKS)]
         summed = keep.tile([P, S], F32, name="summed")
         down = [[psum.tile([P, PAIR], F32, name=f"down{b}{u}", tag=f"act{2 * u + b}") for u in range(2)] for b in range(BLOCKS)]
 
@@ -250,13 +251,12 @@ def tile_picked_modres_glusilu_p_kernel(
         second_product(0, h_codes[:], h_scales[:])
         h_homes.append(shared.tile([P, PAIR * PACK], BF16, name="h1", offset=0, align_bytes=64)[:])
         hidden(2)
-        hidden(3)
         apply_gate(1, first_pair)
+        hidden(3)
+        sum_and_scatter_on_scalar(first_pair)
         last_h_codes, last_h_scales = quantize(h_homes[1], PAIR, "h1")
         second_product(1, last_h_codes[:], last_h_scales[:])
-        sum_and_scatter_on_scalar(first_pair)
         apply_gate(0, first_pair)
-        nc.vector.tensor_copy(old[0][:, S - CHUNK :], res_tiles[0][:].indirect(offsets[:, (S - CHUNK) // 16 :]))
         apply_gate(1, second_pair)
         apply_gate(0, second_pair)
         sum_and_scatter_on_scalar(second_pair)

@@ -199,13 +199,14 @@ def tile_picked_modres_glusilu_p_kernel(
         )
         gates.append(gate_values(3, late[:, S:]))
 
-        old = [keep.tile([P, S], F32, name=f"old{b}")[:] for b in range(BLOCKS)]
+        tail_home = keep.tile([P, 2 * S - CHUNK], F32, name="tail_home")
+        old = [tail_home[:, :S], keep.tile([P, S], F32, name="old1")[:]]
         nc.scalar.activation(old[1], res_tiles[1][:].indirect(offsets[:]), ACT.Copy)
-        nc.scalar.activation(old[0], res_tiles[0][:].indirect(offsets[:]), ACT.Copy)
+        nc.scalar.activation(old[0][:, : S - CHUNK], res_tiles[0][:].indirect(offsets[:, : (S - CHUNK) // 16]), ACT.Copy)
 
         ups = [first_product(w3_q, c, f"up{c}", range(PACK) if c == 0 else range(PACK - 1, -1, -1)) for c in range(CHUNKS)]
         h_homes = [keep.tile([P, PAIR * PACK], BF16, name="h0", align_bytes=64)[:]]
-        gated = [keep.tile([P, S], F32, name=f"gated{b}")[:] for b in range(BLOCKS)]
+        gated = [keep.tile([P, S], F32, name="gated0")[:], tail_home[:, S - CHUNK :]]
         summed = keep.tile([P, S], F32, name="summed")
         down = [[psum.tile([P, PAIR], F32, name=f"down{b}{u}", tag=f"act{2 * u + b}") for u in range(2)] for b in range(BLOCKS)]
 
@@ -251,12 +252,13 @@ def tile_picked_modres_glusilu_p_kernel(
         second_product(0, h_codes[:], h_scales[:])
         h_homes.append(shared.tile([P, PAIR * PACK], BF16, name="h1", offset=0, align_bytes=64)[:])
         hidden(2)
-        apply_gate(1, first_pair)
         hidden(3)
-        sum_and_scatter_on_scalar(first_pair)
+        apply_gate(1, first_pair)
         last_h_codes, last_h_scales = quantize(h_homes[1], PAIR, "h1")
         second_product(1, last_h_codes[:], last_h_scales[:])
+        sum_and_scatter_on_scalar(first_pair)
         apply_gate(0, first_pair)
+        nc.vector.tensor_copy(old[0][:, S - CHUNK :], res_tiles[0][:].indirect(offsets[:, (S - CHUNK) // 16 :]))
         apply_gate(1, second_pair)
         apply_gate(0, second_pair)
         sum_and_scatter_on_scalar(second_pair)

@@ -23,6 +23,7 @@ CHUNK = 128
 CHUNKS = S // CHUNK
 PAIR = 2 * CHUNK
 BLOCKS = N // P
+LENT = 64
 W2_ON_SCALAR = 64
 VEC_M = 80
 VEC_M_FIRST = 72
@@ -199,14 +200,13 @@ def tile_picked_modres_glusilu_p_kernel(
         )
         gates.append(gate_values(3, late[:, S:]))
 
-        tail_home = keep.tile([P, 2 * S - CHUNK], F32, name="tail_home")
-        old = [tail_home[:, :S], keep.tile([P, S], F32, name="old1")[:]]
+        old = [keep.tile([P, S], F32, name=f"old{b}")[:] for b in range(BLOCKS)]
         nc.scalar.activation(old[1], res_tiles[1][:].indirect(offsets[:]), ACT.Copy)
-        nc.scalar.activation(old[0][:, : S - CHUNK], res_tiles[0][:].indirect(offsets[:, : (S - CHUNK) // 16]), ACT.Copy)
+        nc.scalar.activation(old[0], res_tiles[0][:].indirect(offsets[:]), ACT.Copy)
 
         ups = [first_product(w3_q, c, f"up{c}", range(PACK) if c == 0 else range(PACK - 1, -1, -1)) for c in range(CHUNKS)]
         h_homes = [keep.tile([P, PAIR * PACK], BF16, name="h0", align_bytes=64)[:]]
-        gated = [keep.tile([P, S], F32, name="gated0")[:], tail_home[:, S - CHUNK :]]
+        gated = [keep.tile([P, S], F32, name=f"gated{b}")[:] for b in range(BLOCKS)]
         summed = keep.tile([P, S], F32, name="summed")
         down = [[psum.tile([P, PAIR], F32, name=f"down{b}{u}", tag=f"act{2 * u + b}") for u in range(2)] for b in range(BLOCKS)]
 
@@ -229,16 +229,18 @@ def tile_picked_modres_glusilu_p_kernel(
         def apply_gate(b, cols):
             nc.vector.tensor_tensor(gated[b][:, cols], down[b][cols.start // PAIR][:], gate_all[:, cols], ALU.mult)
 
-        def sum_and_scatter_on_scalar(cols):
+        def add_old(cols):
             nc.vector.tensor_tensor(summed[:, cols], gated[1][:, cols], old[1][:, cols], ALU.add)
+
+        def scatter_on_scalar(cols):
             entries = offsets[:, cols.start // 16 : cols.stop // 16]
             nc.scalar.activation(res_tiles[1][:].indirect(entries), summed[:, cols], ACT.Copy)
 
-        def scatter_on_vector(first, last):
+        def scatter_on_vector(b, first, last):
             nc.vector.tensor_tensor(
-                res_tiles[0][:].indirect(offsets[:, first // 16 : last // 16]),
-                old[0][:, first:last],
-                gated[0][:, first:last],
+                res_tiles[b][:].indirect(offsets[:, first // 16 : last // 16]),
+                old[b][:, first:last],
+                gated[b][:, first:last],
                 ALU.add,
             )
 
@@ -256,12 +258,14 @@ def tile_picked_modres_glusilu_p_kernel(
         apply_gate(1, first_pair)
         last_h_codes, last_h_scales = quantize(h_homes[1], PAIR, "h1")
         second_product(1, last_h_codes[:], last_h_scales[:])
-        sum_and_scatter_on_scalar(first_pair)
+        add_old(slice(LENT, PAIR))
+        scatter_on_vector(1, 0, LENT)
+        scatter_on_scalar(slice(LENT, PAIR))
         apply_gate(0, first_pair)
-        nc.vector.tensor_copy(old[0][:, S - CHUNK :], res_tiles[0][:].indirect(offsets[:, (S - CHUNK) // 16 :]))
         apply_gate(1, second_pair)
         apply_gate(0, second_pair)
-        sum_and_scatter_on_scalar(second_pair)
-        scatter_on_vector(0, S)
+        add_old(second_pair)
+        scatter_on_scalar(second_pair)
+        scatter_on_vector(0, 0, S)
         nc.sync.dma_start(out[P:, :], res_tiles[1][:])
         nc.sync.dma_start(out[:P, :], res_tiles[0][:])

@@ -26,7 +26,7 @@ BLOCKS = N // P
 LENT = 64
 W2_ON_SCALAR = 64
 VEC_M = 80
-VEC_M_FIRST = 72
+VEC_M_FIRST = 56
 VEC_M_BUSY = 80
 VEC_M_LAST = 38
 
@@ -71,9 +71,9 @@ def tile_picked_modres_glusilu_p_kernel(
 
         w1_raw = [keep.tile([P, PACK, H], F32, name="w1_raw0", align_bytes=64)]
         w1_first = w1[:K_PASS, :].rearrange("(p j) c -> p j c", j=PACK)
-        nc.sync.dma_start(w1_raw[0][:, :2], w1_first[:, :2])
+        nc.sync.dma_start(w1_raw[0][:, :3], w1_first[:, :3])
         load_scales((2, 3))
-        nc.sync.dma_start(w1_raw[0][:, 2:], w1_first[:, 2:])
+        nc.sync.dma_start(w1_raw[0][:, 3:], w1_first[:, 3:])
         w1_raw.append(load_rows(w1, 1, "w1_raw1"))
         w3_raw = [load_rows(w3, 0, "w3_raw0")]
         w3_last = keep.tile([P, PACK * H], F32, name="w3_last", tag="w3_last", align_bytes=64)
@@ -125,7 +125,7 @@ def tile_picked_modres_glusilu_p_kernel(
             nc.vector.tensor_copy(x_codes[g][:], word_tables[g][:].indirect(offsets[:]))
         x_sc = keep.tile([P, S], U8, name="x_sc", align_bytes=64)
         nc.vector.tensor_copy(x_sc[:], scale_table[:].indirect(offsets[:]))
-        w1_q = [quantize_first(round_first(w1_raw[0], "w1_0", VEC_M_FIRST, 1), "w1_0", 1)]
+        w1_q = [quantize_first(round_first(w1_raw[0], "w1_0", VEC_M_FIRST, 1), "w1_0", 2)]
         w1_q.append(quantize_first(round_first(w1_raw[1], "w1_1", VEC_M, 2), "w1_1", 2))
 
         w3_q = [quantize_first(round_first(w3_raw[0], "w3_0", VEC_M_BUSY, 2), "w3_0", 2)]

from contextlib import ExitStack

import concourse.mybir as mybir

K, T, S, H, N = 1024, 1024, 512, 512, 256
FLOPS = 2 * S * (2 * K * H + H * N)

F32 = mybir.dt.float32
BF16 = mybir.dt.bfloat16
I32 = mybir.dt.int32
U32 = mybir.dt.uint32
U16 = mybir.dt.uint16
U8 = mybir.dt.uint8
FP8X4 = mybir.dt.float8_e4m3fn_x4
ACT = mybir.ActivationFunctionType
ALU = mybir.AluOpType

P = 128
PACK = 4
K_PASS = P * PACK
PASSES = K // K_PASS
CHUNK = 128
CHUNKS = S // CHUNK
PAIR = 2 * CHUNK
BLOCKS = N // P
LENT = 64
W2_ON_SCALAR = 64
VEC_M = 80
VEC_M_FIRST = 56
VEC_M_BUSY = 80
VEC_M_LAST = 38


def tile_picked_modres_glusilu_p_kernel(
    tc, x_words, x_scales, gate, res, w1, w3, w2, offs, out
):
    nc = tc.nc
    with ExitStack() as ctx:
        keep = ctx.enter_context(tc.tile_pool(name="keep", bufs=1))
        shared = ctx.enter_context(tc.tile_pool(name="shared", bufs=1))
        psum = ctx.enter_context(tc.psum_pool(name="psum", bufs=1))

        offsets = keep.tile([P, S // 16], U16, name="offsets")

        scale_table = keep.tile([P, T], U8, name="scale_table", align_bytes=64)
        nc.vector.memset(scale_table[:].bitcast(I32), 0)
        warm = keep.tile([P, 2], F32, name="warm")
        nc.gpsimd.memset(warm[:, 0:1], 0.0)
        nc.scalar.activation(warm[:, 1:2], warm[:, 0:1], ACT.Silu)

        word_tables = [keep.tile([P, T], U32, name=f"word_table{g}", align_bytes=64) for g in range(PASSES)]

        def load_words(g):
            nc.sync.dma_start(word_tables[g][:].bitcast(I32), x_words[g].rearrange("p n t -> p (n t)").bitcast(I32))

        load_words(0)
        nc.sync.dma_start(offsets[:], offs)

        def load_scales(rows):
            for r in rows:
                for g in range(PASSES):
                    nc.sync.dma_start(scale_table[4 * g + r : P : 32, :].bitcast(I32), x_scales[g, r:16:4, :].bitcast(I32))

        load_scales((0, 1))
        load_words(1)

        def load_rows(w, g, name):
            raw = keep.tile([P, PACK, w.shape[1]], F32, name=name, tag=name, align_bytes=64)
            nc.sync.dma_start(raw[:], w[g * K_PASS : (g + 1) * K_PASS, :].rearrange("(p j) c -> p j c", j=PACK))
            return raw

        w1_raw = [keep.tile([P, PACK, H], F32, name="w1_raw0", align_bytes=64)]
        w1_first = w1[:K_PASS, :].rearrange("(p j) c -> p j c", j=PACK)
        nc.sync.dma_start(w1_raw[0][:, :3], w1_first[:, :3])
        load_scales((2, 3))
        nc.sync.dma_start(w1_raw[0][:, 3:], w1_first[:, 3:])
        w1_raw.append(load_rows(w1, 1, "w1_raw1"))
        w3_raw = [load_rows(w3, 0, "w3_raw0")]
        w3_last = keep.tile([P, PACK * H], F32, name="w3_last", tag="w3_last", align_bytes=64)
        w3_halves = w3_last[:].rearrange("p (u j c) -> p u j c", u=2, j=PACK)
        for u in range(2):
            rows = w3[K_PASS:, u * H // 2 : (u + 1) * H // 2]
            nc.sync.dma_start(w3_halves[:, u], rows.rearrange("(p j) c -> p j c", j=PACK))
        w2_raw = shared.tile([P, PACK, N], F32, name="w2_raw", offset=0, align_bytes=64)
        nc.sync.dma_start(w2_raw[:], w2.rearrange("(p j) c -> p j c", j=PACK))
        res_tiles = [keep.tile([P, T], F32, name=f"res{b}") for b in range(BLOCKS)]
        nc.sync.dma_start(res_tiles[1][:], res[P : 2 * P, :])
        gate_all = keep.tile([P, S], F32, name="gate_all")
        nc.sync.dma_start(gate_all[:, :PAIR], gate[:, :PAIR])
        nc.sync.dma_start(res_tiles[0][:], res[0:P, :])
        nc.sync.dma_start(gate_all[:, PAIR:], gate[:, PAIR:])

        def quantize(grouped, width, name):
            codes = keep.tile([P, width], U32, name=name + "_codes", align_bytes=64)
            scales = keep.tile([P, width], U8, name=name + "_scales", align_bytes=64)
            nc.vector.quantize_mx(out=codes[:].bitcast(FP8X4), scales=scales[:], in_=grouped)
            return codes, scales

        def round_first(raw, name, on_vector, steps):
            grouped = keep.tile([P, H * PACK], BF16, name=name + "_bf16", tag=name + "_bf16", align_bytes=64)
            dst = grouped[:].rearrange("p (t m j) -> p m j t", t=PACK, j=PACK)
            src = raw[:].rearrange("p j (m t) -> p m j t", t=PACK)
            width = PACK // steps
            for i in range(steps):
                tiles = slice(i * width, (i + 1) * width)
                nc.vector.tensor_copy(dst[:, :on_vector, :, tiles], src[:, :on_vector, :, tiles])
                nc.scalar.copy(dst[:, on_vector:, :, tiles], src[:, on_vector:, :, tiles])
            return grouped

        def quantize_first(grouped, name, steps):
            codes = keep.tile([P, H], U32, name=name + "_codes", tag=name + "_codes", align_bytes=64)
            scales = keep.tile([P, H], U8, name=name + "_scales", align_bytes=64)
            width = PACK // steps
            for i in range(steps):
                chans = slice(i * width * P, (i + 1) * width * P)
                nc.vector.quantize_mx(
                    out=codes[:, chans].bitcast(FP8X4),
                    scales=scales[:, chans],
                    in_=grouped[:, chans.start * PACK : chans.stop * PACK],
                )
            return codes, scales

        x_codes = [keep.tile([P, S], U32, name=f"x_codes{g}", align_bytes=64) for g in range(PASSES)]
        for g in range(PASSES):
            nc.vector.tensor_copy(x_codes[g][:], word_tables[g][:].indirect(offsets[:]))
        x_sc = keep.tile([P, S], U8, name="x_sc", align_bytes=64)
        nc.vector.tensor_copy(x_sc[:], scale_table[:].indirect(offsets[:]))
        w1_q = [quantize_first(round_first(w1_raw[0], "w1_0", VEC_M_FIRST, 1), "w1_0", 2)]
        w1_q.append(quantize_first(round_first(w1_raw[1], "w1_1", VEC_M, 2), "w1_1", 2))

        w3_q = [quantize_first(round_first(w3_raw[0], "w3_0", VEC_M_BUSY, 2), "w3_0", 2)]

        def first_product(w_q, c, tag, last_order):
            bank = psum.tile([P, PACK, CHUNK], F32, name=tag, tag=tag)
            cols = slice(c * CHUNK, (c + 1) * CHUNK)
            steps = [(t, 0) for t in range(PACK)] + [(t, 1) for t in last_order]
            for t, g in steps:
                chans = slice(t * P, (t + 1) * P)
                codes, scales = w_q[g]
                nc.tensor.matmul_mx(
                    out=bank[:, t, :],
                    lhsT=codes[:, chans].bitcast(FP8X4),
                    lhsT_scale=scales[:, chans],
                    rhs=x_codes[g][:, cols].bitcast(FP8X4),
                    rhs_scale=x_sc[4 * g :, cols],
                    start=(t, g) == steps[0],
                    stop=(t, g) == steps[-1],
                )
            return bank[:].rearrange("p t n -> p n t")

        early = keep.tile([P, 2 * S], F32, name="silu_early", tag="w3_raw0", align_bytes=64)

        def gate_values(c, home):
            pre = first_product(w1_q, c, f"act{c}", range(PACK))
            act = home.rearrange("p (n t) -> p n t", t=PACK)
            nc.scalar.activation(act, pre, ACT.Silu)
            return act

        gates = [gate_values(c, home) for c, home in enumerate((early[:, :S], early[:, S:]))]
        grouped = keep.tile([P, H * PACK], BF16, name="w3_1_bf16", tag="w3_1_bf16", align_bytes=64)
        dst = grouped[:].rearrange("p (t m j) -> p m j t", t=PACK, j=PACK)
        dst = dst.rearrange("p (u m) j t -> p u m j t", u=2)
        src = w3_halves.rearrange("p u j (m t) -> p u m j t", t=PACK)
        last_codes = keep.tile([P, H], U32, name="w3_1_codes", align_bytes=64)
        last_scales = keep.tile([P, H], U8, name="w3_1_scales", align_bytes=64)

        def quantize_half(u):
            for t in range(PACK):
                chans = slice(t * P + u * P // 2, t * P + (u + 1) * P // 2)
                nc.vector.quantize_mx(
                    out=last_codes[:, chans].bitcast(FP8X4),
                    scales=last_scales[:, chans],
                    in_=grouped[:, chans.start * PACK : chans.stop * PACK],
                )

        tile_pairs = (slice(0, 2), slice(2, PACK))
        for tiles in tile_pairs:
            nc.vector.tensor_copy(dst[:, 0, :, :, tiles], src[:, 0, :, :, tiles])
        quantize_half(0)
        for tiles in tile_pairs:
            nc.vector.tensor_copy(dst[:, 1, :VEC_M_LAST, :, tiles], src[:, 1, :VEC_M_LAST, :, tiles])
            nc.scalar.copy(dst[:, 1, VEC_M_LAST:, :, tiles], src[:, 1, VEC_M_LAST:, :, tiles])
        quantize_half(1)
        w3_q.append((last_codes, last_scales))

        late = keep.tile([P, 2 * S], F32, name="silu_late", tag="w3_last", align_bytes=64)
        gates.append(gate_values(2, late[:, :S]))
        w2_bf16 = keep.tile([P, N * PACK], BF16, name="w2_bf16", tag="w3_1_bf16", align_bytes=64)
        nc.scalar.copy(
            w2_bf16[:, : W2_ON_SCALAR * PACK].rearrange("p (c i j) -> p c j i", i=4, j=PACK),
            w2_raw[:, :, :W2_ON_SCALAR].rearrange("p j (c i) -> p c j i", i=4),
        )
        nc.gpsimd.tensor_scalar(
            w2_bf16[:, W2_ON_SCALAR * PACK :].rearrange("p (c j) -> p c j", j=PACK),
            w2_raw[:, :, W2_ON_SCALAR:].rearrange("p j c -> p c j"),
            1.0,
            0.0,
            ALU.mult,
            ALU.add,
        )
        gates.append(gate_values(3, late[:, S:]))

        old = [keep.tile([P, S], F32, name=f"old{b}")[:] for b in range(BLOCKS)]
        nc.scalar.activation(old[1], res_tiles[1][:].indirect(offsets[:]), ACT.Copy)
        nc.scalar.activation(old[0], res_tiles[0][:].indirect(offsets[:]), ACT.Copy)

        ups = [first_product(w3_q, c, f"up{c}", range(PACK) if c == 0 else range(PACK - 1, -1, -1)) for c in range(CHUNKS)]
        h_homes = [keep.tile([P, PAIR * PACK], BF16, name="h0", align_bytes=64)[:]]
        gated = [keep.tile([P, S], F32, name=f"gated{b}")[:] for b in range(BLOCKS)]
        summed = keep.tile([P, S], F32, name="summed")
        down = [[psum.tile([P, PAIR], F32, name=f"down{b}{u}", tag=f"act{2 * u + b}") for u in range(2)] for b in range(BLOCKS)]

        def hidden(c):
            h = h_homes[c // 2].rearrange("p (n t) -> p n t", t=PACK)
            nc.vector.tensor_tensor(h[:, c % 2 * CHUNK : (c % 2 + 1) * CHUNK, :], ups[c], gates[c], ALU.mult)

        def second_product(u, codes, scales):
            for b in (1, 0):
                nc.tensor.matmul_mx(
                    out=down[b][u][:],
                    lhsT=w2_codes[:, b * P : (b + 1) * P].bitcast(FP8X4),
                    lhsT_scale=w2_scales[:, b * P : (b + 1) * P],
                    rhs=codes.bitcast(FP8X4),
                    rhs_scale=scales,
                    start=True,
                    stop=True,
                )

        def apply_gate(b, cols):
            nc.vector.tensor_tensor(gated[b][:, cols], down[b][cols.start // PAIR][:], gate_all[:, cols], ALU.mult)

        def add_old(cols):
            nc.vector.tensor_tensor(summed[:, cols], gated[1][:, cols], old[1][:, cols], ALU.add)

        def scatter_on_scalar(cols):
            entries = offsets[:, cols.start // 16 : cols.stop // 16]
            nc.scalar.activation(res_tiles[1][:].indirect(entries), summed[:, cols], ACT.Copy)

        def scatter_on_vector(b, first, last):
            nc.vector.tensor_tensor(
                res_tiles[b][:].indirect(offsets[:, first // 16 : last // 16]),
                old[b][:, first:last],
                gated[b][:, first:last],
                ALU.add,
            )

        first_pair, second_pair = slice(0, PAIR), slice(PAIR, S)
        hidden(0)
        hidden(1)
        w2_codes, w2_scales = quantize(w2_bf16[:], N, "w2")
        h_codes = shared.tile([P, PAIR], U32, name="h0_codes", offset=2 * PAIR * PACK, align_bytes=64)
        h_scales = keep.tile([P, PAIR], U8, name="h0_scales", align_bytes=64)
        nc.vector.quantize_mx(out=h_codes[:].bitcast(FP8X4), scales=h_scales[:], in_=h_homes[0])
        second_product(0, h_codes[:], h_scales[:])
        h_homes.append(shared.tile([P, PAIR * PACK], BF16, name="h1", offset=0, align_bytes=64)[:])
        hidden(2)
        hidden(3)
        apply_gate(1, first_pair)
        last_h_codes, last_h_scales = quantize(h_homes[1], PAIR, "h1")
        second_product(1, last_h_codes[:], last_h_scales[:])
        add_old(slice(LENT, PAIR))
        scatter_on_vector(1, 0, LENT)
        scatter_on_scalar(slice(LENT, PAIR))
        apply_gate(0, first_pair)
        apply_gate(1, second_pair)
        apply_gate(0, second_pair)
        add_old(second_pair)
        scatter_on_scalar(second_pair)
        scatter_on_vector(0, 0, S)
        nc.sync.dma_start(out[P:, :], res_tiles[1][:])
        nc.sync.dma_start(out[:P, :], res_tiles[0][:])
